import numpy as np, ml_dtypes
CORES = [1,5,17,21,33,37,49,53]
N = 8
BF = ml_dtypes.bfloat16
P, L, B, T = 3072, 256, 2, 3
def skew(rng, n, hot):
    u = rng.random((N, 8, n))
    return np.take_along_axis(hot, np.minimum((P * u * u).astype(np.int64), P - 1), 2)
def parts(rng):
    x = rng.integers(0, 256, (N, 8, 16, P)); h = rng.integers(0, 256, (N, 8, 16, L))
    hot = np.argsort(rng.random((N, 8, P)), axis=2)
    pl = skew(rng, 16 * P, np.roll(hot, -1, axis=0)).reshape(N, 8, 16, P); kt = skew(rng, 16 * L, hot).reshape(N, 8, 16, L)
    nx = np.argsort(rng.random((N, 8, P)), axis=2); nx[:, 1::2] = skew(rng, P, hot)[:, 1::2]
    bm = rng.integers(0, P, (N, 8, L))
    th = np.stack([rng.integers(750, 1001, (N, 8)), rng.integers(900, 1251, (N, 8))], axis=2)
    return x, pl, nx, kt, h, bm, th
def pack(x, pl, nx, kt, h, bm, th):
    return {"xp": np.ascontiguousarray(x.reshape(N, 128, P)).astype(np.float32).astype(BF), "pl": np.ascontiguousarray(pl.reshape(N, 128, P)).astype(np.int32), "nx": np.ascontiguousarray(nx).astype(np.int32),
            "kt": np.ascontiguousarray(kt.reshape(N, 128, L)).astype(np.int32), "hm": np.ascontiguousarray(h.reshape(N, 128, L)).astype(np.float32).astype(BF), "bm": np.ascontiguousarray(bm).astype(np.int32), "th": np.ascontiguousarray(th).astype(np.int32)}
def setup_inputs(rng):
    return pack(*parts(rng))
def setup_inputs_spread(rng):
    x, pl, nx, kt, h, bm, th = parts(rng)
    x = np.minimum((rng.random(x.shape) * np.exp2(8.1 * rng.random((N, 8, 1, P)))).astype(np.int64), 255)
    h = np.minimum((rng.random(h.shape) * np.exp2(8.1 * rng.random((N, 8, 1, L)))).astype(np.int64), 255)
    th = np.minimum(np.exp2(12.0 * rng.random((N, 8, 2))).astype(np.int64), 4095); th[:, 2, 0] = rng.integers(300, 1200, N)
    hot = np.argsort(rng.random((N, 8, P)), axis=2); u = rng.random((N, 8, 16 * P)) ** 4
    pl = np.take_along_axis(np.roll(hot, -1, axis=0), np.minimum((P * u).astype(np.int64), P - 1), 2).reshape(N, 8, 16, P)
    nx[:, ::3] = skew(rng, P, hot)[:, ::3]
    return pack(x, pl, nx, kt, h, bm, th)
def edge(rng, n):
    return np.where(rng.random((N, 8, n)) < 0.7, (P - 1) * rng.integers(0, 2, (N, 8, n)), rng.integers(0, P, (N, 8, n)))
def setup_inputs_ends(rng):
    k = rng.integers(0, 5, (N, 8, 1, P)); x = np.where(k == 0, 0, np.where(k == 1, 255, 255 * rng.integers(0, 2, (N, 8, 16, P))))
    k = rng.integers(0, 8, (N, 8, 1, L)); h = np.where(k == 0, 0, np.where(k == 1, 255, np.where(k == 2, 127, 255 * rng.integers(0, 2, (N, 8, 16, L)))))
    x[..., 0] = 0; x[..., P - 1] = 255
    pl = edge(rng, 16 * P).reshape(N, 8, 16, P); kt = edge(rng, 16 * L).reshape(N, 8, 16, L); nx = edge(rng, P); bm = edge(rng, L)
    th = 4095 * np.ones((N, 8, 2), np.int64); th[:, :, 1] = 4095 * rng.integers(0, 2, (N, 8))
    for q in range(N):
        o = rng.permutation(7); th[q, o[:2], 0] = 0; th[q, o[2], 1] = 0; th[q, 7, 1] = 4095
        for g in range(8):
            if (q + g) % 4 == 0: nx[q, g, 0] = P - 1; nx[q, g, P - 1] = 0
            else: nx[q, g, 0] = rng.integers(7, P - 1); nx[q, g, P - 1] = rng.integers(7, P - 1)
        for g in (int(o[3]), 7):
            a = x[q, g]; a[:, [P - 1, 1, 2, 3]] = 255; a[:, [0, 4, 5, 6]] = 0
            kt[q, g, :, L - 1] = np.tile(np.array([P - 1, 1, 2, 3]), 4); h[q, g, :, L - 1] = 0
            kt[q, g, :, L - 2] = np.tile(np.array([5, 0, 4, 6]), 4); h[q, g, :, L - 2] = 255
    return pack(x, pl, nx, kt, h, bm, th)
def setup_inputs_corners(rng):
    x, pl, nx, kt, h, bm, th = parts(rng); pp = np.arange(P); kk = np.arange(16)[:, None]; li = np.arange(L)[None, :]
    for q in range(N):
        for g in range(8):
            b = (q - 1) % N; w = (g + q) % 8
            if w == 0: nx[q, g] = pp; th[q, g] = (4095, 4095)
            elif w == 1: nx[q, g] = pp ^ 1; th[q, g] = (1200, 0)
            elif w == 2:
                nx[q, g] = (pp + 1) % P; kt[q, g] = (P - 40 + li + kk) % P; pl[b, g] = (pp[None, :] + kk) % P; th[q, g] = (4095, 4095)
            elif w == 3:
                nx[q, g] = P - 1; bm[q, g] = np.where(li[0] % 3 == 0, 0, np.where(li[0] % 3 == 1, P - 1, li[0])); th[q, g] = (2000, 4095)
            elif w == 4:
                z = (0, P - 1, P // 2)[q % 3]; kt[q, g] = z; pl[b, g] = z; th[q, g] = (4095, 1100)
            elif w == 5:
                x[q, g] = x[q, g][:, pp - (pp & 7)]; th[q, g] = (2000, 1000)
                kt[q, g] = 8 * rng.integers(0, P // 8, (1, L)) + rng.integers(0, 8, (16, L)); pl[b, g] = 8 * rng.integers(0, P // 8, (1, P)) + rng.integers(0, 8, (16, P))
            elif w == 6:
                th[q, g] = (0, 4095); bm[q, g, 0] = 0; bm[q, g, L - 1] = P - 1; nx[q, g, 0] = 0
            else:
                kt[q, g] = (li + kk) & 15; pl[b, g] = rng.integers(0, 16, (16, P)); nx[q, g, :16] = (np.arange(16) + 1) & 15; th[q, g] = (4095, 4095)
    x[:, 7] = 255; h[:, 7] = 255; nx[:, 7] = pp; th[:, 7] = 4095
    kt[:, 7] = np.where(li < 31, 16 + li, (li + kk) & 15); pl[:, 7] = kk; pl[:, 7, :, 16:47] = 64 + np.arange(31)
    for q in range(N):
        b = (q - 1) % N; assert np.sum(np.any(~np.isin(pl[b, 7][:, kt[b, 7, 0]], kt[q, 7, 0]), axis=0)) == 31
    return pack(x, pl, nx, kt, h, bm, th)
def setup_inputs_ties(rng):
    x, pl, nx, kt, h, bm, th = parts(rng); t = rng.integers(40, 101, (N, 8, 1))
    far = t + np.where(rng.random((N, 8, P)) < 0.5, rng.integers(-1, 2, (N, 8, P)), rng.integers(0, 34, (N, 8, P)))
    x = 100 + np.where(np.arange(16)[:, None] == rng.integers(0, 16, (N, 8, 1, P)), far[:, :, None, :], 0)
    h = 100 + np.zeros((N, 8, 16, L), np.int64); h[:, :, 0] += (rng.random((N, 8, L)) < 0.125).astype(np.int64)
    order = np.argsort(far + rng.random(far.shape), axis=2); q = np.array([0.0, 0.2, 0.35, 0.55, 0.7, 0.9])
    def near(n, o):
        a = (P * rng.choice(q, (N, 8, 1, n))).astype(np.int64); i = np.minimum(a + ((P - a) * rng.random((N, 8, 16, n))).astype(np.int64), P - 1)
        return np.take_along_axis(o, i.reshape(N, 8, 16 * n), 2).reshape(N, 8, 16, n)
    kt = near(L, order); pl = near(P, np.roll(order, -1, axis=0))
    th = np.concatenate([t, ((t - 1) >> 1) + t + rng.integers(-1, 2, (N, 8, 1))], axis=2)
    return pack(x, pl, nx, kt, h, bm, th)
def sums(d):
    return (d[None, :] + ((np.arange(16)[:, None] + np.arange(d.shape[0])[None, :]) & 15)) >> 4
def setup_inputs_counts(rng):
    x, pl, nx, kt, h, bm, th = parts(rng); li = np.arange(L); kk = np.arange(16)[:, None]; gs = [int(g) for g in rng.permutation(8)]
    o = np.argsort(rng.random((N, 8, P)), axis=2)[:, :, :5 * L].reshape(N, 8, 5, L)
    h[:, gs[:6]] = 0
    for w in range(5):
        g = gs[w]; r = rng.permutation(L)
        for q in range(N):
            a, b, c, e, f = o[q, g]; a2, b2, c2, e2, f2 = o[(q + 1) % N, g]; pq = pl[q, g]; nq = nx[q, g]; kq = kt[q, g]
            if w < 2: t = 16 * int(rng.integers(128, 250)) + int(rng.choice(np.array([3, 4, 5, 11, 12, 13])))
            else: t = int(rng.integers(64, 4001))
            d = t + 40 + rng.integers(0, 41, P)
            if w == 0:
                d = t - 17 + rng.integers(0, 35, P); d[a] = t - 17 + li % 35; kq[:] = a; th[q, g, 0] = t
            elif w == 1:
                d = rng.integers(0, 4081, P); d[a] = 0; d[b] = t - 17 + li % 35; nq[a] = b; kq[:] = a; th[q, g] = (int(rng.integers(64, 4001)), t)
            elif w == 2:
                d[a] = 0; d[b] = t - 2 + li % 36; nq[a] = f; pq[:, a] = b2; kq[:] = a; th[q, g] = (t, 0)
            elif w == 3:
                m = r[:40]; v = r[40:53]
                d[a] = 0; d[b] = 0; d[c[m]] = t - 2 + np.arange(40) % 36
                nq[a] = f; nq[b] = f; nq[a[v]] = a[v]
                pq[:, a] = f2; pq[:, a[m]] = b2[m]; pq[:, a[v]] = a2[v][(np.arange(13) + kk) % 13]; pq[:, b[m]] = c2[m]
                kq[:] = a; th[q, g] = (t, 0)
            else:
                m = r[:52]; z = r[52:]
                d[a[m]] = 0; d[e[z]] = t - 2 + np.arange(L - 52) % 36
                nq[a[m[:-1]]] = a[m[1:]]; nq[a[m[-1]]] = f[0]; nq[b] = c; bm[q, g] = b
                pq[:, a] = f2; pq[:, b] = f2; pq[:, f] = f2; pq[:, c] = e2
                kq[:] = f; kq[:, m] = a[m]; th[q, g] = (t, 0)
            x[q, g] = sums(d)
    g = gs[5]; x[:, g] = 0; nx[:, g] = np.arange(P); th[:, g] = 4095
    kt[:, g] = np.where(li[None, :] < 31, 16 + li[None, :], (li[None, :] + kk) & 15); pl[:, g] = kk; pl[:, g, :, 16:47] = 64 + np.arange(31)
    return pack(x, pl, nx, kt, h, bm, th)
def check_inputs(d):
    bad = []
    for k, hi in (("xp", 255), ("pl", P - 1), ("nx", P - 1), ("kt", P - 1), ("hm", 255), ("bm", P - 1), ("th", 4095)):
        v = np.asarray(d[k]).astype(np.float64)
        if not (np.min(v) >= 0 and np.max(v) <= hi): bad.append("range of " + k)
        if k in ("xp", "hm") and np.any(v != np.floor(v)): bad.append("whole numbers of " + k)
    return bad
def pick(a, ix):
    return np.take_along_axis(a, ix[:, :, None, :], 3)
def mark(flags, y, go):
    a, g, i = np.nonzero(go); flags[a, g, y[a, g, i]] = True
def reference(xp, pl, nx, kt, hm, bm, th):
    x = xp.astype(np.float32).astype(np.int64).reshape(N, 8, 16, P); par = pl.astype(np.int64).reshape(N, 8, 16, P); nxt = nx.astype(np.int64)
    k = kt.astype(np.int64).reshape(N, 8, 16, L); h = hm.astype(np.float32).astype(np.int64).reshape(N, 8, 16, L)
    b = bm.astype(np.int64); t1 = th.astype(np.int64)[:, :, 0:1]; t2 = th.astype(np.int64)[:, :, 1:2]
    j = np.tile(np.arange(P, dtype=np.int64), (N, 8, 1)); eaten = np.zeros((N, 8, P), bool); a = np.zeros((N, 8, 1), np.int64)
    for t in range(T):
        c = np.take_along_axis(j, k.reshape(N, 8, 16 * L), 2).reshape(N, 8, 16, L)
        void = np.take_along_axis(eaten, c.reshape(N, 8, 16 * L), 2).reshape(N, 8, 16, L)
        d = np.stack([np.add.reduce(np.abs(pick(x, c[:, :, i]) - h), axis=2) for i in range(16)], axis=2)
        d = np.where(void, 2 ** 20, d)
        w = np.argmin(d, axis=2)[:, :, None, :]
        hit = np.take_along_axis(d, w, 2)[:, :, 0] < t1 + (a & 31)
        y = np.where(hit, np.take_along_axis(c, w, 2)[:, :, 0], np.take_along_axis(j, b, 2))
        new = np.zeros((N, 8, P), bool); go = hit
        h = np.where(go[:, :, None, :], (h + pick(x, y)) >> 1, h); mark(new, y, go)
        for s in range(B):
            n = np.take_along_axis(j, np.take_along_axis(nxt, y, 2), 2); xn = pick(x, n)
            go = go & ~np.take_along_axis(eaten, n, 2) & (np.add.reduce(np.abs(xn - h), axis=2) <= t2)
            y = np.where(go, n, y); h = np.where(go[:, :, None, :], (h + xn) >> 1, h); mark(new, y, go)
        b = np.take_along_axis(nxt, y, 2); a = np.add.reduce(hit.astype(np.int64), axis=2, keepdims=True)
        j = np.where(new, nxt, j); eaten = eaten | new
        j = np.take_along_axis(j, j, 2)
        if t < T - 1:
            k = np.roll(pick(par, y), 1, axis=0); h = np.roll(h, 1, axis=0)
    return {"yj": j.astype(np.float32), "yh": h.reshape(N, 128, L).astype(np.float32).astype(BF), "yb": b.astype(np.float32)}

@@ -1,0 +1,561 @@
+from concourse.mybir import dt, AluOpType, AxisListType, ActivationFunctionType
+
+OP = AluOpType
+FN = ActivationFunctionType
+P, L = 3072, 256
+S16 = 2.0 ** -16
+BIG = 16384.0
+VOID = 8192.0
+MAGIC = 12582912.0
+
+SCRATCH = {
+    "xsb": ("sbuf", [128, P], "bfloat16"),
+    "plw": ("sbuf", [128, P], "int32"),
+    "tj0": ("sbuf", [128, P], "bfloat16"),
+    "tj1": ("sbuf", [128, P], "bfloat16"),
+    "tj2": ("sbuf", [128, P], "bfloat16"),
+    "ev": ("sbuf", [128, P], "float32"),
+    "x1": ("sbuf", [128, P], "float32"),
+    "x2": ("sbuf", [128, P], "float32"),
+    "dw": ("sbuf", [128, 4096], "float32"),
+    "ab": ("sbuf", [128, 16, 256], "bfloat16"),
+    "hrep": ("sbuf", [128, 4096], "bfloat16"),
+    "lh": ("sbuf", [128, 48 * 128], "bfloat16"),
+    "rh": ("sbuf", [128, 48 * 208], "bfloat16"),
+    "kti": ("sbuf", [128, 256], "int32"),
+    "k0": ("sbuf", [128, 256], "uint16"),
+    "ks0": ("sbuf", [128, 256], "uint16"),
+    "ks1": ("sbuf", [128, 256], "uint16"),
+    "kl1": ("sbuf", [128, 256], "uint16"),
+    "kl2": ("sbuf", [128, 256], "uint16"),
+    "h0": ("sbuf", [128, 256], "bfloat16"),
+    "hl1": ("sbuf", [128, 256], "bfloat16"),
+    "hl2": ("sbuf", [128, 256], "bfloat16"),
+    "hx0": ("sbuf", [128, 256], "bfloat16"),
+    "hx1": ("sbuf", [128, 256], "bfloat16"),
+    "hs0": ("sbuf", [128, 256], "bfloat16"),
+    "hs1": ("sbuf", [128, 256], "bfloat16"),
+    "hs2": ("sbuf", [128, 256], "bfloat16"),
+    "off": ("sbuf", [128, 16], "uint16"),
+    "ml": ("sbuf", [128, 16], "uint16"),
+    "yl": ("sbuf", [128, 16], "uint16"),
+    "bl": ("sbuf", [128, 16], "uint16"),
+    "jl": ("sbuf", [128, 384], "uint16"),
+    "sc": ("sbuf", [128, 256], "float32"),
+    "i0": ("sbuf", [128, 16], "int32"),
+    "i1": ("sbuf", [128, 16], "int32"),
+    "i2": ("sbuf", [128, 16], "int32"),
+    "w": ("sbuf", [128, 256], "float32"),
+    "a1": ("sbuf", [128, 256], "bfloat16"),
+    "rs": ("sbuf", [128, 768], "bfloat16"),
+    "qb": ("sbuf", [128, 256], "int32"),
+    "gob": ("sbuf", [128, 768], "bfloat16"),
+    "qn": ("sbuf", [128, 96], "float32"),
+    "nb": ("sbuf", [128, 48], "float32"),
+    "yy": ("sbuf", [128, 32], "float32"),
+    "gw": ("sbuf", [128, 32], "float32"),
+    "t32": ("sbuf", [128, 32], "float32"),
+    "y1": ("sbuf", [128, 16], "float32"),
+    "y2": ("sbuf", [128, 16], "float32"),
+    "rb": ("sbuf", [128, 256], "bfloat16"),
+    "ry": ("sbuf", [128, 256], "bfloat16"),
+    "g16": ("sbuf", [128, 256], "float32"),
+    "kq": ("sbuf", [128, 256], "int32"),
+    "kk": ("sbuf", [128, 256], "float32"),
+    "sgc": ("sbuf", [128, 208], "float32"),
+    "dfc": ("sbuf", [128, 192], "float32"),
+    "cnt": ("sbuf", [128, 192], "float32"),
+    "v15": ("sbuf", [128, 192], "float32"),
+    "x15": ("sbuf", [128, 192], "bfloat16"),
+    "nxb": ("sbuf", [128, 192], "int32"),
+    "nqi": ("sbuf", [128, 192], "int32"),
+    "nt": ("sbuf", [128, 192], "float32"),
+    "nt2": ("sbuf", [128, 192], "float32"),
+    "nx2": ("sbuf", [128, 384], "bfloat16"),
+    "j2": ("sbuf", [128, 384], "bfloat16"),
+    "j2n": ("sbuf", [128, 384], "bfloat16"),
+    "dd": ("sbuf", [128, 384], "float32"),
+    "d2": ("sbuf", [128, 384], "float32"),
+    "bmr": ("sbuf", [128, 256], "int32"),
+    "bqi": ("sbuf", [128, 256], "int32"),
+    "bt": ("sbuf", [128, 256], "float32"),
+    "bt2": ("sbuf", [128, 256], "float32"),
+    "bqs": ("sbuf", [128, 256], "bfloat16"),
+    "bns": ("sbuf", [128, 256], "bfloat16"),
+    "thi": ("sbuf", [128, 2], "int32"),
+    "thf": ("sbuf", [128, 2], "float32"),
+    "thr": ("sbuf", [128, 8], "float32"),
+    "acn": ("sbuf", [128, 1], "float32"),
+    "aci": ("sbuf", [128, 1], "int32"),
+    "acj": ("sbuf", [128, 1], "int32"),
+    "ybs": ("sbuf", [128, 256], "float32"),
+    "yjs": ("sbuf", [128, 192], "float32"),
+    "rix": ("sbuf", [128, 193], "bfloat16"),
+    "ri": ("sbuf", [128, 192], "bfloat16"),
+    "im": ("sbuf", [128, 160], "bfloat16"),
+    "igr": ("sbuf", [128, 128], "bfloat16"),
+    "kcb": ("sbuf", [128, 256], "bfloat16"),
+    "pci": ("sbuf", [128, 1], "int32"),
+    "ria": ("sbuf", [128, 1], "int32"),
+    "bsi": ("sbuf", [128, 16], "int32"),
+    "bs": ("sbuf", [128, 16], "int32"),
+    "cols": ("sbuf", [128, 32], "float32"),
+    "zs": ("sbuf", [128, 7 * 144], "bfloat16"),
+    "ids": ("sbuf", [128, 5 * 128], "bfloat16"),
+    "bo": ("sbuf", [128, 128], "bfloat16"),
+    "bof": ("sbuf", [128, 128], "float32"),
+    "mrow": ("sbuf", [128, 128], "bfloat16"),
+    "lb": ("sbuf", [128, 128], "bfloat16"),
+    "rst": ("sbuf", [128, 256], "float32"),
+    "n512": ("sbuf", [128, 48], "bfloat16"),
+}
+for _b in range(8):
+    SCRATCH["ps%d" % _b] = ("psum", [128, 512], "float32")
+SEMAPHORES = ["sV", "sS", "sP", "sG", "ls", "ah1", "ak1", "ah2", "ak2"] + ["d%d" % _i for _i in range(40)]
+
+ZK, ZQ, ZN, ZMA, ZMI, ZG, ZY = range(7)
+I1, I192, I1S, I16, ING = range(5)
+
+
+def make(g, T):
+    eng = {"V": g.vector, "S": g.scalar, "P": g.tensor, "G": g, "Y": g.sync}
+    total, known, clock, hist, waited = {}, {q: {} for q in eng}, {}, {}, {}
+
+    def need(q, deps):
+        for sem, val in sorted(deps, key=lambda d: -d[1]):
+            if known[q].get(sem, 0) >= val:
+                continue
+            eng[q].wait_ge(T.sem[sem], val)
+            waited[sem] = max(waited.get(sem, 0), val)
+            for s, v in clock[(sem, val)].items():
+                if known[q].get(s, 0) < v:
+                    known[q][s] = v
+
+    def conflicts(q, reads, writes, noself):
+        deps = {}
+        for accs, wr in ((reads, False), (writes, True)):
+            for name, lo, hi in accs:
+                ps = name[:2] == "ps"
+                for (tok, eq, ew, elo, ehi) in hist.get(name, []):
+                    over = lo < ehi and elo < hi
+                    if eq == q and tok[0][0] == "s":
+                        c = over and (ew or wr) and not (noself and wr)
+                    else:
+                        c = (over and (ew or wr)) or (ps and eq != q)
+                    if c:
+                        deps[tok[0]] = max(deps.get(tok[0], 0), tok[1])
+        return list(deps.items())
+
+    def record(tok, q, reads, writes):
+        for accs, wr in ((reads, False), (writes, True)):
+            for name, lo, hi in accs:
+                hs = hist.setdefault(name, [])
+                if wr:
+                    hs[:] = [e for e in hs if not (lo <= e[3] and e[4] <= hi)]
+                else:
+                    hs[:] = [e for e in hs if not (e[0][0] == tok[0] and not e[2] and lo <= e[3] and e[4] <= hi)]
+                hs.append((tok, q, wr, lo, hi))
+
+    def token(q, sem, n):
+        total[sem] = total.get(sem, 0) + n
+        tok = (sem, total[sem])
+        clock[tok] = dict(known[q])
+        clock[tok][sem] = total[sem]
+        return tok
+
+    def op(q, calls, reads, writes, noself=False):
+        if not isinstance(calls, list):
+            calls = [calls]
+        need(q, conflicts(q, reads, writes, noself))
+        sem = "s" + q
+        for c in calls:
+            c(eng[q]).then_inc(T.sem[sem], 1)
+            tok = token(q, sem, 1)
+        record(tok, q, reads, writes)
+
+    nd = [0]
+
+    def dma(q, out, in_, reads, writes):
+        need(q, conflicts(q, reads, writes, False))
+        sem = "d%d" % nd[0]
+        nd[0] += 1
+        eng[q].dma_start(out, in_).then_inc(T.sem[sem], 16)
+        record(token(q, sem, 16), q, reads, writes)
+
+    def remote(fn, n, reads):
+        need("G", conflicts("G", reads, [], False))
+        fn()
+        record(token("G", "ls", n), "G", reads, [])
+
+    def arrive(sem, n, name, width):
+        total[sem] = n
+        clock[(sem, n)] = {sem: n}
+        hist.setdefault(name, []).append(((sem, n), "R", True, 0, width))
+
+    def finish():
+        for sem, n in total.items():
+            if waited.get(sem, 0) < n:
+                g.wait_ge(T.sem[sem], n)
+
+    return op, dma, remote, arrive, finish
+
+
+def rank_program(g, core, T, topo):
+    rank = T.rank_of(core)
+    if rank is None:
+        return
+    n_ranks = len(T.cores)
+    nxt, prv = T.cores[(rank + 1) % n_ranks], T.cores[(rank - 1) % n_ranks]
+    op, dma, remote, arrive, finish = make(g, T)
+    ps = [T["ps%d" % b] for b in range(8)]
+
+    def R(name, lo=0, hi=None):
+        return (name, lo, hi if hi is not None else 1 << 20)
+
+    def ts(out, i, s1, s2, o0, o1, reads, writes):
+        if s2 is None:
+            op("V", lambda e: e.tensor_scalar(out, i, s1, None, o0), reads, writes)
+        else:
+            op("V", lambda e: e.tensor_scalar(out, i, s1, s2, o0, o1), reads, writes)
+
+    def tt(out, a, b, o, reads, writes):
+        op("V", lambda e: e.tensor_tensor(out, a, b, o), reads, writes)
+
+    def cp(out, i, reads, writes):
+        op("V", lambda e: e.tensor_copy(out, i), reads, writes)
+
+    def act(out, i, fn, reads, writes, **kw):
+        op("S", lambda e: e.activation(out, i, fn, **kw), reads, writes)
+
+    def fill(ap, c, name):
+        op("V", lambda e: e.memset(ap, c), [], [R(name)])
+
+    def mm(specs, reads, writes):
+        op("P", [lambda e, s=s: e.matmul(s[0], s[1], s[2], s[3], s[4]) for s in specs], reads, writes, noself=True)
+
+    def group(out, pairs):
+        n = len(pairs)
+        return [(out, a, b, j == 0, j == n - 1) for j, (a, b) in enumerate(pairs)]
+
+    def z(s, r):
+        return T.zs[:, 144 * s + 15 - r: 144 * s + 15 - r + 128]
+
+    def idm(s):
+        return T.ids[:, 128 * s: 128 * s + 128]
+
+    def wrapped(s, src, stop, lo=0):
+        return [(z(s, r), src[:, lo + r: stop: 16]) for r in range(16)]
+
+    dma("S", T.nxb[:], T.nx[:], [], [R("nxb")])
+    dma("Y", T.xsb[:, 0:1536], T.xp[:, 0:1536], [], [R("xsb", 0, 1536)])
+    dma("Y", T.xsb[:, 1536:3072], T.xp[:, 1536:3072], [], [R("xsb", 1536, 3072)])
+    dma("S", T.h0[:], T.hm[:], [], [R("h0")])
+    dma("S", T.kti[:], T.kt[:], [], [R("kti")])
+    fill(T.thi[:], 0, "thi")
+    fill(T.bmr[:], 0, "bmr")
+    dma("Y", T.thi[0::16, :], T.th[:], [], [R("thi")])
+    dma("Y", T.bmr[0::16, :], T.bm[:], [], [R("bmr")])
+    dma("Y", T.x15[:], T.xp[15::16, :], [], [R("x15")])
+
+    def iota(out, pattern, base, cm, name):
+        op("G", lambda e: e.iota(out, pattern, base, cm, allow_small_or_imprecise_dtypes=True), [], [R(name)])
+    iota(T.pci[:], [[0, 1]], 0, 1, "pci")
+    iota(T.ri[:], [[1, 192]], 0, 0, "ri")
+    iota(T.im[:], [[1, 160]], 0, 0, "im")
+    iota(T.igr[:], [[16, 8], [0, 16]], 0, 0, "igr")
+    iota(T.kcb[:], [[0, 16], [1, 16]], 0, 0, "kcb")
+    iota(T.bsi[:], [[256, 16]], 0, 0, "bsi")
+    iota(T.rix[:], [[1, 193]], -1, 0, "rix")
+    fill(T.tj0[:], 0.0, "tj0")
+    C = lambda j: T.cols[:, j:j + 1]
+    RC = lambda j: R("cols", j, j + 1)
+    CP_, CR, CG, CGZ, CRS, W0, TA, TB = 0, 1, 2, 3, 4, 8, 24, 25
+    ts(T.ria[:], T.pci[:], 15, None, OP.bitwise_and, None, [R("pci")], [R("ria")])
+    cp(C(CP_), T.pci[:], [R("pci")], [RC(CP_)])
+    cp(C(CR), T.ria[:], [R("ria")], [RC(CR)])
+    tt(C(CG), C(CP_), C(CR), OP.subtract, [RC(CP_), RC(CR)], [RC(CG)])
+    ts(C(CRS), C(CR), S16, None, OP.mult, None, [RC(CR)], [RC(CRS)])
+    ts(T.j2[:, 0:192], T.ri[:], 0.0, C(CRS), OP.mult, OP.add, [R("ri"), RC(CRS)], [R("j2", 0, 192)])
+    ts(T.j2[:, 192:384], T.ri[:], S16, None, OP.mult, None, [R("ri")], [R("j2", 192, 384)])
+    dma("S", T.tj0[0::16, :], T.j2[:, 0:192], [R("j2", 0, 192), R("tj0")], [R("tj0r0")])
+    dma("Y", T.tj0[1::16, :], T.j2[:, 192:384], [R("j2", 192, 384), R("tj0")], [R("tj0r1")])
+    ts(T.nqi[:], T.nxb[:], 1.0 / 192, -95.5 / 192, OP.mult, OP.add, [R("nxb")], [R("nqi")])
+    ts(T.nx2[:, 0:192], T.nqi[:], S16, None, OP.mult, None, [R("nqi")], [R("nx2", 0, 192)])
+    ts(T.nt[:], T.nqi[:], -192.0, None, OP.mult, None, [R("nqi")], [R("nt")])
+    dma("S", T.tj0[2::16, :], T.nx2[:, 0:192], [R("nx2", 0, 192), R("tj0")], [R("tj0r2")])
+    tt(T.nt2[:], T.nt[:], T.nxb[:], OP.add, [R("nxb"), R("nt")], [R("nt2")])
+    ts(T.nx2[:, 192:384], T.nt2[:], S16, None, OP.mult, None, [R("nt2")], [R("nx2", 192, 384)])
+    dma("Y", T.tj0[3::16, :], T.nx2[:, 192:384], [R("nx2", 192, 384), R("tj0")], [R("tj0r3")])
+    TJ0 = [R("tj0"), R("tj0r0"), R("tj0r1"), R("tj0r2"), R("tj0r3")]
+    for j, v in ((I1, 1.0), (I1S, 65536.0), (I192, 192.0 * 65536), (I16, 16.0 * 65536), (ING, -BIG)):
+        ts(idm(j), T.im[:, 0:128], C(CP_), v, OP.is_equal, OP.mult, [R("im"), RC(CP_)], [R("ids", 128 * j, 128 * j + 128)])
+    ts(C(CGZ), C(CG), 15.0, None, OP.add, None, [RC(CG)], [RC(CGZ)])
+    ts(T.bo[:], T.igr[:], C(CG), None, OP.is_equal, None, [R("igr"), RC(CG)], [R("bo")])
+    ts(T.lb[:], T.im[:, 0:128], C(CG), None, OP.subtract, None, [R("im"), RC(CG)], [R("lb")])
+    ts(T.rst[:], T.kcb[:], 0.0, 1e9, OP.is_equal, OP.mult, [R("kcb")], [R("rst")])
+
+    def col2(j, terms):
+        (r0, v0) = terms[0]
+        if len(terms) == 1:
+            ts(C(j), C(CR), float(r0), v0, OP.is_equal, OP.mult, [RC(CR)], [RC(j)])
+            return
+        (r1, v1) = terms[1]
+        ts(C(TA), C(CR), float(r0), v0, OP.is_equal, OP.mult, [RC(CR)], [RC(TA)])
+        ts(C(TB), C(CR), float(r1), v1, OP.is_equal, OP.mult, [RC(CR)], [RC(TB)])
+        tt(C(j), C(TA), C(TB), OP.add, [RC(TA), RC(TB)], [RC(j)])
+    u = 65536.0
+    ts(C(W0 + ZK), C(CR), 0.0, 16.0, OP.mult, OP.add, [RC(CR)], [RC(W0 + ZK)])
+    col2(W0 + ZQ, [(0, u)])
+    col2(W0 + ZN, [(1, u)])
+    col2(W0 + ZMA, [(2, 192 * u), (3, u)])
+    col2(W0 + ZMI, [(2, u), (3, 16 * u)])
+    col2(W0 + ZG, [(0, 512.0)])
+    col2(W0 + ZY, [(0, 192 * u), (1, u)])
+    for s in (ZK, ZQ, ZMA, ZN, ZG, ZMI, ZY):
+        ts(T.zs[:, 144 * s:144 * s + 144], T.im[:, 0:144], C(CGZ), C(W0 + s), OP.is_equal, OP.mult,
+           [R("im"), RC(CGZ), RC(W0 + s)], [R("zs", 144 * s, 144 * s + 144)])
+    Z = lambda s: R("zs", 144 * s, 144 * s + 144)
+    ID = lambda s: R("ids", 128 * s, 128 * s + 128)
+    ts(T.i0[:, 0:1], T.ria[:], 16, None, OP.mult, None, [R("ria")], [R("i0")])
+    cp(C(TA), T.i0[:, 0:1], [R("i0")], [RC(TA)])
+    ts(T.bs[:], T.bsi[:], C(TA), None, OP.add, None, [R("bsi"), RC(TA)], [R("bs")])
+    cp(T.k0[:], T.kti[:], [R("kti")], [R("k0")])
+
+    def make_hrep(h):
+        for k in range(16):
+            o, i = T.hrep[:, k::16], T[h][:]
+            if k % 3 != 2:
+                cp(o, i, [R(h)], [R("hrepv")] if k == 0 else [R("hrepv%d" % k)])
+            else:
+                act(o, i, FN.Copy, [R(h)], [R("hreps%d" % k)])
+    HREP = [R("hrepv")] + [R("hrepv%d" % k) for k in range(1, 16) if k % 3 != 2] + [R("hreps%d" % k) for k in range(16) if k % 3 == 2]
+    make_hrep("h0")
+
+    for c in range(6):
+        b = 2 + c
+        sl = slice(512 * c, 512 * c + 512)
+        mm(group(ps[b][:], [(idm(I1), T.xsb[:, sl]), (idm(I1), T.tj0[:, sl])]),
+           [ID(I1), R("xsb", 512 * c, 512 * c + 512)] + TJ0, [R("ps%d" % b)])
+        if c % 2:
+            act(T.ev[:, sl], ps[b][:], FN.Copy, [R("ps%d" % b)], [R("ev", 512 * c, 512 * c + 512)])
+        else:
+            cp(T.ev[:, sl], ps[b][:], [R("ps%d" % b)], [R("ev", 512 * c, 512 * c + 512)])
+    dma("Y", T.plw[:], T.pl[:], [R("ev")], [R("plw")])
+
+    def late_setup():
+        ts(T.bof[:], T.igr[:], C(CG), None, OP.is_equal, None, [R("igr"), RC(CG)], [R("bof")])
+        cp(T.thf[:], T.thi[:], [R("thi")], [R("thf")])
+        mm(group(ps[4][:, 160:162], [(T.bof[:], T.thf[:])]), [R("bof"), R("thf")], [R("ps4", 160, 162)])
+        ts(T.thr[:, 0:1], ps[4][:, 160:161], -0.5, None, OP.add, None, [R("ps4", 160, 162)], [R("thr", 0, 1)])
+        ts(T.thr[:, 1:2], ps[4][:, 161:162], 0.5 - BIG, None, OP.add, None, [R("ps4", 160, 162)], [R("thr", 1, 2)])
+        cp(T.thr[:, 2:3], T.thr[:, 0:1], [R("thr", 0, 1)], [R("thr", 2, 3)])
+        fill(T.n512[:], -512.0, "n512")
+        ts(T.bqi[:], T.bmr[:], 1.0 / 192, -95.5 / 192, OP.mult, OP.add, [R("bmr")], [R("bqi")])
+        ts(T.bqs[:], T.bqi[:], S16, None, OP.mult, None, [R("bqi")], [R("bqs")])
+        ts(T.bt[:], T.bqi[:], -192.0, None, OP.mult, None, [R("bqi")], [R("bt")])
+        tt(T.bt2[:], T.bt[:], T.bmr[:], OP.add, [R("bt"), R("bmr")], [R("bt2")])
+        ts(T.bns[:], T.bt2[:], S16, None, OP.mult, None, [R("bt2")], [R("bns")])
+        mm(group(ps[4][:, 96:112], wrapped(ZQ, T.bqs, 256)) + group(ps[4][:, 112:128], wrapped(ZQ, T.bns, 256)),
+           [R("bqs"), R("bns"), Z(ZQ)], [R("ps4", 96, 128)])
+        ts(T.mrow[:], T.igr[:], C(CG), C(W0 + ZMA), OP.is_equal, OP.mult, [R("igr"), RC(CG), RC(W0 + ZMA)], [R("mrow")])
+        tt(T.dd[:], T.nx2[:], T.j2[:], OP.subtract, [R("nx2"), R("j2")], [R("dd")])
+        ts(T.d2[:], T.dd[:], 1.0 / VOID, None, OP.mult, None, [R("dd")], [R("d2")])
+        cp(T.v15[:], T.x15[:], [R("x15")], [R("v15")])
+        fill(T.tj1[:], 0.0, "tj1")
+
+    TJ1 = [R("tj1"), R("tj1r0"), R("tj1r1")]
+    for hop in (1, 2):
+        x = len(topo.engines(prv, core))
+        arrive("ah%d" % hop, x, "hl%d" % hop, 256)
+        arrive("ak%d" % hop, x, "kl%d" % hop, 256)
+
+    def send(dst, src, sem):
+        rid, pid = topo.addr(nxt)[:2]
+        remote(lambda: g.remote_dma(T[dst][:], T[src][:], T.sem[sem], T.sem.ls, pid, rid, topo.mask(core, nxt)),
+               len(topo.engines(core, nxt)), [R(src)])
+
+    def tj_piece(j):
+        w = 24
+        act(T.tj2[:, 16 * w * j:16 * w * (j + 1)], T.tj1[:, 0:P].indirect(T.jl[:, w * j:w * (j + 1)]), FN.Identity,
+            TJ1 + [R("jl", w * j, w * (j + 1))], [R("tj2", 16 * w * j, 16 * w * (j + 1))])
+
+    for t in range(3):
+        last = t == 2
+        xt, xn = (T.ev, "ev") if t == 0 else (T.x2, "x2")
+        kn = ("k0", "kl1", "kl2")[t]
+        hn = ("h0", "hl1", "hl2")[t]
+        for c in range(4):
+            if t and c == 0:
+                tj_piece(0), tj_piece(1)
+            sl = slice(1024 * c, 1024 * c + 1024)
+            tt(T.dw[:, sl], xt[:, 0:P].indirect(T[kn][:, 64 * c:64 * c + 64]), T.hrep[:, sl], OP.subtract,
+               [R(xn), R(kn)] + HREP, [R("dw", 1024 * c, 1024 * c + 1024)])
+            for a in range(4 * c, 4 * c + 4, 4):
+                act(T.ab[:, a:a + 4, :], T.dw[:, sl], FN.Abs, [R("dw", 1024 * c, 1024 * c + 1024)],
+                    [R("ab", c, c + 1)])
+            mm(group(ps[0][:, 64 * c:64 * c + 64],
+                     [(idm(I1), T.kcb[:, 64 * c:64 * c + 64])] + [(z(ZK, r), T.ab[:, 4 * c:4 * c + 4, 16 * r:16 * r + 16]) for r in range(16)]),
+               [R("ab", c, c + 1), R("kcb"), Z(ZK), ID(I1)], [R("ps0", 64 * c, 64 * c + 64)])
+            if t:
+                tj_piece(2 + c)
+        if t == 0:
+            late_setup()
+        op("V", lambda e: e.tensor_tensor_scan(T.sc[:], T.rst[:], ps[0][:, 0:256], 1e9, OP.max, OP.min),
+           [R("rst"), R("ps0")], [R("sc")])
+        cp(T.i0[:], T.sc[:, 15::16], [R("sc")], [R("i0")])
+        ts(T.i1[:], T.i0[:], 15, None, OP.bitwise_and, None, [R("i0")], [R("i1")])
+        tt(T.i2[:], T.i1[:], T.bs[:], OP.add, [R("i1"), R("bs")], [R("i2")])
+        cp(T.off[:], T.i2[:], [R("i2")], [R("off")])
+        cp(T.w[:], T.dw[:, 0:4096].indirect(T.off[:]), [R("dw"), R("off")], [R("w")])
+        if t:
+            tj_piece(6), tj_piece(7)
+        zm = ZMA if t == 0 else ZMI
+        qn_done = []
+
+        def digits(lo, hi, go_lo):
+            n = 16 * (hi - lo)
+            base = 32 * lo
+            mm(group(ps[4][:, base:base + n],
+                     [(idm(I1), T.n512[:, 0:n])] + wrapped(ZQ, T.rs, 256 * hi, 256 * lo) + wrapped(ZG, T.gob, 256 * hi, 256 * lo))
+               + group(ps[4][:, base + n:base + 2 * n], wrapped(ZN, T.rs, 256 * hi, 256 * lo)),
+               [R("rs", 256 * lo, 256 * hi), R("gob", 256 * lo, 256 * hi), R("n512"), ID(I1), Z(ZQ), Z(ZG), Z(ZN)],
+               [R("ps4", base, base + 2 * n)])
+            cp(T.qn[:, base:base + 2 * n], ps[4][:, base:base + 2 * n], [R("ps4", base, base + 2 * n)], [R("qn", base, base + 2 * n)])
+            ts(T.nb[:, 16 * lo:16 * hi], T.qn[:, base + n:base + 2 * n], -1.0, 0.5, OP.mult, OP.add,
+               [R("qn", base, base + 2 * n)], [R("nb", 16 * lo, 16 * hi)])
+            return base, base + n
+
+        first = {"V": True, "S": True}
+        stops = {"V": 32 + 8, "S": 47}
+
+        def count(items, qcol, ncol, s_items):
+            for j, it in enumerate(items):
+                lsl = slice(128 * it, 128 * it + 128)
+                ts(T.lh[:, lsl], T.lb[:], T.qn[:, qcol + j:qcol + j + 1], None, OP.is_equal, None,
+                   [R("lb"), R("qn", qcol, qcol + len(items))], [R("lh", 128 * it, 128 * it + 128)])
+                if it in s_items:
+                    rsl = slice(208 * it, 208 * it + 193)
+                    act(T.rh[:, rsl], T.rix[:], FN.Sign, [R("rix"), R("nb", it, it + 1)], [R("rh", 208 * it, 208 * it + 208)],
+                        bias=T.nb[:, it:it + 1])
+                    out, key, rg = ps[0][:, 0:193], "S", "ps0"
+                else:
+                    rsl = slice(208 * it, 208 * it + 192)
+                    ts(T.rh[:, rsl], T.ri[:], T.qn[:, ncol + j:ncol + j + 1], None, OP.is_equal, None,
+                       [R("ri"), R("qn", ncol, ncol + len(items))], [R("rh", 208 * it, 208 * it + 208)])
+                    out, key, rg = ps[5][:, 0:192], "V", "ps5"
+                mm([(out, T.lh[:, lsl], T.rh[:, rsl], first[key], it == last_item[key])],
+                   [R("lh", 128 * it, 128 * it + 128), R("rh", 208 * it, 208 * it + 208)], [R(rg)])
+                first[key] = False
+        s_set = set(range(2, 32, 5)) | set(range(0, 32, 5)) | set(range(33, 48, 5)) | set(range(35, 48, 5))
+        last_item = {"S": max(s_set), "V": max(i for i in range(48) if i not in s_set)}
+
+        def pick(lo, qcol, ncol):
+            qs, ns = T.qn[:, qcol:qcol + 16], T.qn[:, ncol:ncol + 16]
+            rq = [R("qn", qcol, qcol + 16), R("qn", ncol, ncol + 16)]
+            ts(T.gw[:, 0:16], qs, -0.5, None, OP.is_ge, None, rq, [R("gw", 0, 16)])
+            tt(T.t32[:, 0:16], qs, T.yy[:, 0:16], OP.subtract, rq + [R("yy", 0, 16)], [R("t32", 0, 16)])
+            tt(T.t32[:, 16:32], ns, T.yy[:, 16:32], OP.subtract, rq + [R("yy", 16, 32)], [R("t32", 16, 32)])
+            tt(T.t32[:, 0:16], T.t32[:, 0:16], T.gw[:, 0:16], OP.mult, [R("t32", 0, 16), R("gw", 0, 16)], [R("t32", 0, 16)])
+            tt(T.t32[:, 16:32], T.t32[:, 16:32], T.gw[:, 0:16], OP.mult, [R("t32", 16, 32), R("gw", 0, 16)], [R("t32", 16, 32)])
+            tt(T.yy[:], T.yy[:], T.t32[:], OP.add, [R("t32"), R("yy")], [R("yy")])
+
+        for s in range(3):
+            c0 = 256 * s
+            rsl = slice(c0, c0 + 256)
+            hin = (hn, "hx0", "hx1")[s]
+            hout = ("hx0", "hx1", "hs%d" % t)[s]
+            act(T.a1[:], T.w[:], FN.Abs, [R("w")], [R("a1")])
+            if s:
+                mm([(ps[1][:, 0:256], idm(ING), T.gob[:, c0 - 256:c0], True, False)], [R("gob", c0 - 256, c0), ID(ING)], [R("ps1")])
+            ts(ps[6][:, 0:256], T.w[:], MAGIC, MAGIC, OP.add, OP.subtract, [R("w")], [R("ps6", 0, 256)])
+            tt(T.rs[:, rsl], T.w[:], ps[6][:, 0:256], OP.subtract, [R("w"), R("ps6", 0, 256)], [R("rs", c0, c0 + 256)])
+            mm([(ps[1][:, 0:256], T.bo[:], T.a1[:], s == 0, True)], [R("a1"), R("bo")], [R("ps1")])
+            if s < 2:
+                mm(group(ps[3][:, 0:16], wrapped(zm, T.rs, c0 + 256, c0)), [R("rs", c0, c0 + 256), Z(zm)], [R("ps3")])
+            ts(T.qb[:], T.w[:], 0.5, -0.25, OP.mult, OP.add, [R("w")], [R("qb")])
+            th = T.thr[:, 2:3] if s == 0 else T.thr[:, 1:2]
+            ts(ps[2][:, 0:256], ps[1][:, 0:256], th, None, OP.is_le, None, [R("ps1"), R("thr", 1, 3)], [R("ps2", 0, 256)])
+            tt(ps[2][:, 256:512], T.qb[:], ps[2][:, 0:256], OP.mult, [R("qb"), R("ps2", 0, 256)], [R("ps2", 256, 512)])
+            tt(T[hout][:], T[hin][:], ps[2][:, 256:512], OP.add, [R(hin), R("ps2", 256, 512)], [R(hout)])
+            if s < 2:
+                cp(T.ml[:], ps[3][:, 0:16], [R("ps3")], [R("ml")])
+            if s == 0:
+                act(T.gob[:, rsl], ps[2][:, 0:256], FN.Copy, [R("ps2", 0, 256)], [R("gob", c0, c0 + 256), R("acn")], accum_out=T.acn[:])
+            else:
+                act(T.gob[:, rsl], ps[2][:, 0:256], FN.Copy, [R("ps2", 0, 256)], [R("gob", c0, c0 + 256)])
+            if s < 2:
+                tt(T.w[:], xt[:, 0:P].indirect(T.ml[:]), T[hout][:], OP.subtract, [R(xn), R("ml"), R(hout)], [R("w")])
+            if s == 1:
+                qa, na = digits(0, 2, 0)
+        if not last:
+            send("hl%d" % (t + 1), "hs%d" % t, "ah%d" % (t + 1))
+        else:
+            dma("Y", T.yh[:], T.hs2[:], [R("hs2")], [R("yh")])
+        if t:
+            act(T.rb[:], T.tj2[:, 0:P].indirect(T.bl[:]), FN.Identity, [R("tj2"), R("bl")], [R("rb")])
+            mm(group(ps[4][:, 96:112], wrapped(ZQ, T.rb, 256)) + group(ps[4][:, 112:128], wrapped(ZN, T.rb, 256)),
+               [R("rb"), Z(ZQ), Z(ZN)], [R("ps4", 96, 128)])
+            mm(group(ps[7][:, 0:192], [(z(ZQ, r), T.tj2[:, r::16]) for r in range(16)])
+               + group(ps[7][:, 192:384], [(z(ZN, r), T.tj2[:, r::16]) for r in range(16)]),
+               [R("tj2"), Z(ZQ), Z(ZN)], [R("ps7")])
+        count(list(range(32)), qa, na, s_set)
+        qc, nc = digits(2, 3, 0)
+        count(list(range(32, 48)), qc, nc, s_set)
+        if t:
+            ts(T.j2[:], ps[7][:, 0:384], S16, None, OP.mult, None, [R("ps7")], [R("j2")])
+            tt(T.dd[:], T.nx2[:], T.j2[:], OP.subtract, [R("nx2"), R("j2")], [R("dd")])
+            ts(T.d2[:], T.dd[:], 1.0 / VOID, None, OP.mult, None, [R("dd")], [R("d2")])
+        act(T.sgc[:, 0:192], ps[0][:, 0:192], FN.Copy, [R("ps0")], [R("sgc")])
+        tt(T.dfc[:], ps[0][:, 1:193], T.sgc[:, 0:192], OP.subtract, [R("ps0"), R("sgc")], [R("dfc")])
+        tt(T.cnt[:], T.dfc[:], ps[5][:, 0:192], OP.add, [R("dfc"), R("ps5")], [R("cnt")])
+        ts(ps[6][:, 0:192], T.cnt[:], 0.5, VOID, OP.is_gt, OP.mult, [R("cnt")], [R("ps6", 0, 192)])
+        if not last:
+            tt(T.v15[:], T.v15[:], ps[6][:, 0:192], OP.add, [R("v15"), R("ps6", 0, 192)], [R("v15")])
+            dma("Y", T.ev[15::16, :], T.v15[:], [R("v15")], [R("ev")])
+        ts(ps[6][:, 192:384], T.cnt[:], 0.5, VOID, OP.is_gt, OP.mult, [R("cnt")], [R("ps6", 192, 384)])
+        tt(ps[2][:, 0:384], T.d2[:], ps[6][:, 0:384], OP.mult, [R("d2"), R("ps6", 0, 384)], [R("ps2", 0, 384)])
+        tt(T.j2n[:], T.j2[:], ps[2][:, 0:384], OP.add, [R("j2"), R("ps2", 0, 384)], [R("j2n")])
+        dma("Y", T.tj1[0::16, :], T.j2n[:, 0:192], [R("j2n"), R("tj1")], [R("tj1r0")])
+        dma("Y", T.tj1[1::16, :], T.j2n[:, 192:384], [R("j2n"), R("tj1")], [R("tj1r1")])
+        mm(group(ps[7][:, 0:192], [(idm(I192), T.j2n[:, 0:192]), (idm(I1S), T.j2n[:, 192:384])])
+           + group(ps[7][:, 192:384], [(idm(I1S), T.j2n[:, 0:192]), (idm(I16), T.j2n[:, 192:384])]),
+           [R("j2n"), ID(I192), ID(I1S), ID(I16)], [R("ps7")])
+        cp(T.jl[:], ps[7][:, 0:384], [R("ps7")], [R("jl")])
+        cp(T.yy[:], ps[4][:, 96:128], [R("ps4", 96, 128)], [R("yy")])
+        pick(0, qa, na)
+        pick(1, qa + 16, na + 16)
+        pick(2, qc, nc)
+        ts(T.y1[:], T.yy[:, 0:16], 192.0, None, OP.mult, None, [R("yy")], [R("y1")])
+        tt(T.y2[:], T.y1[:], T.yy[:, 16:32], OP.add, [R("y1"), R("yy")], [R("y2")])
+        cp(T.yl[:], T.y2[:], [R("y2")], [R("yl")])
+        act(T.ry[:], T.tj0[:, 0:P].indirect(T.yl[:]), FN.Identity, TJ0 + [R("yl")], [R("ry")])
+        if not last:
+            ts(T.g16[:], T.plw[:, 0:P].indirect(T.yl[:]), 16.0, None, OP.mult, None, [R("plw"), R("yl")], [R("g16")])
+            ts(T.kq[:], T.g16[:], 1.0 / 3072, -1528.0 / 3072, OP.mult, OP.add, [R("g16")], [R("kq")])
+            ts(ps[6][:, 0:256], T.kq[:], -3071.0, None, OP.mult, None, [R("kq")], [R("ps6", 0, 256)])
+            tt(T.kk[:], T.g16[:], ps[6][:, 0:256], OP.add, [R("g16"), R("ps6", 0, 256)], [R("kk")])
+            cp(T["ks%d" % t][:], T.kk[:], [R("kk")], [R("ks%d" % t)])
+            send("kl%d" % (t + 1), "ks%d" % t, "ak%d" % (t + 1))
+            mm(group(ps[4][:, 128:144], wrapped(ZMI, T.ry, 256)), [R("ry"), Z(ZMI)], [R("ps4", 128, 144)])
+            cp(T.bl[:], ps[4][:, 128:144], [R("ps4", 128, 144)], [R("bl")])
+            cp(T.aci[:], T.acn[:], [R("acn")], [R("aci")])
+            ts(T.acj[:], T.aci[:], 31, None, OP.bitwise_and, None, [R("aci")], [R("acj")])
+            tt(T.thr[:, 2:3], T.acj[:], T.thr[:, 0:1], OP.add, [R("acj"), R("thr", 0, 1)], [R("thr", 2, 3)])
+            make_hrep("hl%d" % (t + 1))
+            for src, sn, dst, dn, lo in ((T.ev, "ev", T.x1, "x1", 0), (T.x1, "x1", T.x2, "x2", 192)):
+                op("V", lambda e: e.tensor_copy(dst[:, 0:1536], src[:, 0:P].indirect(T.jl[:, lo:lo + 96])),
+                   [R(sn), R("jl", lo, lo + 96)], [R(dn, 0, 1536)])
+                act(dst[:, 1536:3072], src[:, 0:P].indirect(T.jl[:, lo + 96:lo + 192]), FN.Identity,
+                    [R(sn), R("jl", lo + 96, lo + 192)], [R(dn, 1536, 3072)])
+        else:
+            mm(group(ps[1][:, 0:256], [(T.mrow[:], T.ry[:])]), [R("mrow"), R("ry")], [R("ps1")])
+            act(T.ybs[:], ps[1][:, 0:256], FN.Copy, [R("ps1")], [R("ybs")])
+            dma("Y", T.yb[:], T.ybs[0::16, :], [R("ybs")], [R("yb")])
+            op("V", lambda e: e.tensor_copy(T.tj2[:, 0:1536], T.tj1[:, 0:P].indirect(T.jl[:, 0:96])),
+               TJ1 + [R("jl", 0, 96)], [R("tj2", 0, 1536)])
+            act(T.tj2[:, 1536:3072], T.tj1[:, 0:P].indirect(T.jl[:, 96:192]), FN.Identity,
+                TJ1 + [R("jl", 96, 192)], [R("tj2", 1536, 3072)])
+            mm(group(ps[7][:, 0:192], [(z(ZY, r), T.tj2[:, r::16]) for r in range(16)]), [R("tj2"), Z(ZY)], [R("ps7")])
+            cp(T.yjs[:], ps[7][:, 0:192], [R("ps7")], [R("yjs")])
+            dma("Y", T.yj[:], T.yjs[:], [R("yjs")], [R("yj")])
+    finish()

@@ -4,116 +4,35 @@ OP = AluOpType
 FN = ActivationFunctionType
 P, L = 3072, 256
 S16 = 2.0 ** -16
+U = 65536.0
 BIG = 16384.0
 VOID = 8192.0
 MAGIC = 12582912.0
 
-SCRATCH = {
-    "xsb": ("sbuf", [128, P], "bfloat16"),
-    "plw": ("sbuf", [128, P], "int32"),
-    "tj0": ("sbuf", [128, P], "bfloat16"),
-    "tj1": ("sbuf", [128, P], "bfloat16"),
-    "tj2": ("sbuf", [128, P], "bfloat16"),
-    "ev": ("sbuf", [128, P], "float32"),
-    "x1": ("sbuf", [128, P], "float32"),
-    "x2": ("sbuf", [128, P], "float32"),
-    "dw": ("sbuf", [128, 4096], "float32"),
-    "ab": ("sbuf", [128, 16, 256], "bfloat16"),
-    "hrep": ("sbuf", [128, 4096], "bfloat16"),
-    "lh": ("sbuf", [128, 48 * 128], "bfloat16"),
-    "rh": ("sbuf", [128, 48 * 208], "bfloat16"),
-    "kti": ("sbuf", [128, 256], "int32"),
-    "k0": ("sbuf", [128, 256], "uint16"),
-    "ks0": ("sbuf", [128, 256], "uint16"),
-    "ks1": ("sbuf", [128, 256], "uint16"),
-    "kl1": ("sbuf", [128, 256], "uint16"),
-    "kl2": ("sbuf", [128, 256], "uint16"),
-    "h0": ("sbuf", [128, 256], "bfloat16"),
-    "hl1": ("sbuf", [128, 256], "bfloat16"),
-    "hl2": ("sbuf", [128, 256], "bfloat16"),
-    "hx0": ("sbuf", [128, 256], "bfloat16"),
-    "hx1": ("sbuf", [128, 256], "bfloat16"),
-    "hs0": ("sbuf", [128, 256], "bfloat16"),
-    "hs1": ("sbuf", [128, 256], "bfloat16"),
-    "hs2": ("sbuf", [128, 256], "bfloat16"),
-    "off": ("sbuf", [128, 16], "uint16"),
-    "ml": ("sbuf", [128, 16], "uint16"),
-    "yl": ("sbuf", [128, 16], "uint16"),
-    "bl": ("sbuf", [128, 16], "uint16"),
-    "jl": ("sbuf", [128, 384], "uint16"),
-    "sc": ("sbuf", [128, 256], "float32"),
-    "i0": ("sbuf", [128, 16], "int32"),
-    "i1": ("sbuf", [128, 16], "int32"),
-    "i2": ("sbuf", [128, 16], "int32"),
-    "w": ("sbuf", [128, 256], "float32"),
-    "a1": ("sbuf", [128, 256], "bfloat16"),
-    "rs": ("sbuf", [128, 768], "bfloat16"),
-    "qb": ("sbuf", [128, 256], "int32"),
-    "gob": ("sbuf", [128, 768], "bfloat16"),
-    "qn": ("sbuf", [128, 96], "float32"),
-    "nb": ("sbuf", [128, 48], "float32"),
-    "yy": ("sbuf", [128, 32], "float32"),
-    "gw": ("sbuf", [128, 32], "float32"),
-    "t32": ("sbuf", [128, 32], "float32"),
-    "y1": ("sbuf", [128, 16], "float32"),
-    "y2": ("sbuf", [128, 16], "float32"),
-    "rb": ("sbuf", [128, 256], "bfloat16"),
-    "ry": ("sbuf", [128, 256], "bfloat16"),
-    "g16": ("sbuf", [128, 256], "float32"),
-    "kq": ("sbuf", [128, 256], "int32"),
-    "kk": ("sbuf", [128, 256], "float32"),
-    "sgc": ("sbuf", [128, 208], "float32"),
-    "dfc": ("sbuf", [128, 192], "float32"),
-    "cnt": ("sbuf", [128, 192], "float32"),
-    "v15": ("sbuf", [128, 192], "float32"),
-    "x15": ("sbuf", [128, 192], "bfloat16"),
-    "nxb": ("sbuf", [128, 192], "int32"),
-    "nqi": ("sbuf", [128, 192], "int32"),
-    "nt": ("sbuf", [128, 192], "float32"),
-    "nt2": ("sbuf", [128, 192], "float32"),
-    "nx2": ("sbuf", [128, 384], "bfloat16"),
-    "j2": ("sbuf", [128, 384], "bfloat16"),
-    "j2n": ("sbuf", [128, 384], "bfloat16"),
-    "dd": ("sbuf", [128, 384], "float32"),
-    "d2": ("sbuf", [128, 384], "float32"),
-    "bmr": ("sbuf", [128, 256], "int32"),
-    "bqi": ("sbuf", [128, 256], "int32"),
-    "bt": ("sbuf", [128, 256], "float32"),
-    "bt2": ("sbuf", [128, 256], "float32"),
-    "bqs": ("sbuf", [128, 256], "bfloat16"),
-    "bns": ("sbuf", [128, 256], "bfloat16"),
-    "thi": ("sbuf", [128, 2], "int32"),
-    "thf": ("sbuf", [128, 2], "float32"),
-    "thr": ("sbuf", [128, 8], "float32"),
-    "acn": ("sbuf", [128, 1], "float32"),
-    "aci": ("sbuf", [128, 1], "int32"),
-    "acj": ("sbuf", [128, 1], "int32"),
-    "ybs": ("sbuf", [128, 256], "float32"),
-    "yjs": ("sbuf", [128, 192], "float32"),
-    "rix": ("sbuf", [128, 193], "bfloat16"),
-    "ri": ("sbuf", [128, 192], "bfloat16"),
-    "im": ("sbuf", [128, 160], "bfloat16"),
-    "igr": ("sbuf", [128, 128], "bfloat16"),
-    "kcb": ("sbuf", [128, 256], "bfloat16"),
-    "pci": ("sbuf", [128, 1], "int32"),
-    "ria": ("sbuf", [128, 1], "int32"),
-    "bsi": ("sbuf", [128, 16], "int32"),
-    "bs": ("sbuf", [128, 16], "int32"),
-    "cols": ("sbuf", [128, 32], "float32"),
-    "zs": ("sbuf", [128, 7 * 144], "bfloat16"),
-    "ids": ("sbuf", [128, 5 * 128], "bfloat16"),
-    "bo": ("sbuf", [128, 128], "bfloat16"),
-    "bof": ("sbuf", [128, 128], "float32"),
-    "mrow": ("sbuf", [128, 128], "bfloat16"),
-    "lb": ("sbuf", [128, 128], "bfloat16"),
-    "rst": ("sbuf", [128, 256], "float32"),
-    "n512": ("sbuf", [128, 48], "bfloat16"),
-}
+SCRATCH = {}
+
+
+def _sb(dtype, **names):
+    for name, cols in names.items():
+        SCRATCH[name] = ("sbuf", [128] + (list(cols) if isinstance(cols, tuple) else [cols]), dtype)
+
+
+_sb("bfloat16", xsb=P, tj0=P, tj1=P, tj2=P, ab=(16, 256), hrep=4096, oa=6 * 512, sb=6 * 392, h0=256, hl1=256, hl2=256,
+    hx0=256, hx1=256, hs0=256, hs1=256, hs2=256, a1=256, rs=768, gob=768, rb=256, ry=256, x15=192, nx2=384, j2=384,
+    j2n=384, pxd=384, bqs=256, bns=256, flg=400, ri=192, im=240, igr=128, ig64=512, ig49=392, kcb=256, zs=6 * 144, zb=144,
+    ids=5 * 128, bo=128, mrow=128, rha=512, rhg=392, rhb=392, cbi=392, cbw=392, cb=392, pat=512, zro=392, zx=4 * 240, ix=192, idb=192)
+_sb("float32", ev=P, x1=P, x2=P, dw=4096, sc=256, w=256, yg=96, yy0=16, yy1=16, yy2=16, yy3=16, ta=48, tb=48, g16=256,
+    kk=256, sgc=400, v15=192, nt=192, nt2=192, dd=384, d2=384, bt=256, bt2=256, thf=2, thr=8, acn=1, ybs=256, yjs=192,
+    hv=256, cols=40, bof=128, rst=256)
+_sb("int32", hi0=256, hi1=256, plw=P, kti=256, i0=16, i1=16, i2=16, qb=256, kq=256, nxb=192, nqi=192, bmr=256, bqi=256, thi=2, aci=1, acj=1,
+    pci=1, ria=1, pk3=1, pk4=1, bsi=16, bs=16, r16=1)
+_sb("uint16", k0=256, ks0=256, ks1=256, kl1=256, kl2=256, off=16, ml=16, yl=16, bl=16, jl=384)
 for _b in range(8):
     SCRATCH["ps%d" % _b] = ("psum", [128, 512], "float32")
 SEMAPHORES = ["sV", "sS", "sP", "sG", "ls", "ah1", "ak1", "ah2", "ak2"] + ["d%d" % _i for _i in range(40)]
 
-ZK, ZQ, ZN, ZMA, ZMI, ZG, ZY = range(7)
+ZK, ZQ, ZN, ZMA, ZMI, ZY = range(6)
+ZG = ZQ
 I1, I192, I1S, I16, ING = range(5)
 
 
@@ -248,88 +167,122 @@ def rank_program(g, core, T, topo):
 
     dma("S", T.nxb[:], T.nx[:], [], [R("nxb")])
     dma("Y", T.xsb[:, 0:1536], T.xp[:, 0:1536], [], [R("xsb", 0, 1536)])
-    dma("Y", T.xsb[:, 1536:3072], T.xp[:, 1536:3072], [], [R("xsb", 1536, 3072)])
     dma("S", T.h0[:], T.hm[:], [], [R("h0")])
+    dma("Y", T.xsb[:, 1536:3072], T.xp[:, 1536:3072], [], [R("xsb", 1536, 3072)])
     dma("S", T.kti[:], T.kt[:], [], [R("kti")])
+    fill(T.tj0[:], 0.0, "tj0")
     fill(T.thi[:], 0, "thi")
     fill(T.bmr[:], 0, "bmr")
-    dma("Y", T.thi[0::16, :], T.th[:], [], [R("thi")])
-    dma("Y", T.bmr[0::16, :], T.bm[:], [], [R("bmr")])
-    dma("Y", T.x15[:], T.xp[15::16, :], [], [R("x15")])
 
     def iota(out, pattern, base, cm, name):
         op("G", lambda e: e.iota(out, pattern, base, cm, allow_small_or_imprecise_dtypes=True), [], [R(name)])
     iota(T.pci[:], [[0, 1]], 0, 1, "pci")
     iota(T.ri[:], [[1, 192]], 0, 0, "ri")
-    iota(T.im[:], [[1, 160]], 0, 0, "im")
-    iota(T.igr[:], [[16, 8], [0, 16]], 0, 0, "igr")
+    iota(T.ix[:], [[1, 4], [0, 48]], 0, 0, "ix")
+    iota(T.idb[:], [[0, 4], [1, 48]], 0, 0, "idb")
+    iota(T.im[:], [[1, 240]], 0, 0, "im")
     iota(T.kcb[:], [[0, 16], [1, 16]], 0, 0, "kcb")
+    iota(T.igr[:], [[16, 8], [0, 16]], 0, 0, "igr")
     iota(T.bsi[:], [[256, 16]], 0, 0, "bsi")
-    iota(T.rix[:], [[1, 193]], -1, 0, "rix")
-    fill(T.tj0[:], 0.0, "tj0")
+    iota(T.ig64[:], [[16, 8], [0, 64]], 0, 0, "ig64")
+    iota(T.ig49[:], [[16, 8], [0, 49]], 0, 0, "ig49")
+    iota(T.cbw[:], [[0, 8], [1, 49]], 0, 0, "cbw")
+    iota(T.pat[:], [[0, 8], [1, 64]], 0, 0, "pat")
     C = lambda j: T.cols[:, j:j + 1]
     RC = lambda j: R("cols", j, j + 1)
-    CP_, CR, CG, CGZ, CRS, W0, TA, TB = 0, 1, 2, 3, 4, 8, 24, 25
+    CP_, CR, CG, CGZ, CRS, W0, WA, WB, WG, KD, KM, WX, TA = 0, 1, 2, 3, 4, 8, 14, 15, 16, 17, 18, 19, 24
     ts(T.ria[:], T.pci[:], 15, None, OP.bitwise_and, None, [R("pci")], [R("ria")])
     cp(C(CP_), T.pci[:], [R("pci")], [RC(CP_)])
     cp(C(CR), T.ria[:], [R("ria")], [RC(CR)])
-    tt(C(CG), C(CP_), C(CR), OP.subtract, [RC(CP_), RC(CR)], [RC(CG)])
+    ts(idm(I1), T.im[:, 0:128], C(CP_), 1.0, OP.is_equal, OP.mult, [R("im"), RC(CP_)], [R("ids", 0, 128)])
     ts(C(CRS), C(CR), S16, None, OP.mult, None, [RC(CR)], [RC(CRS)])
     ts(T.j2[:, 0:192], T.ri[:], 0.0, C(CRS), OP.mult, OP.add, [R("ri"), RC(CRS)], [R("j2", 0, 192)])
-    ts(T.j2[:, 192:384], T.ri[:], S16, None, OP.mult, None, [R("ri")], [R("j2", 192, 384)])
-    dma("S", T.tj0[0::16, :], T.j2[:, 0:192], [R("j2", 0, 192), R("tj0")], [R("tj0r0")])
-    dma("Y", T.tj0[1::16, :], T.j2[:, 192:384], [R("j2", 192, 384), R("tj0")], [R("tj0r1")])
+    ts(T.pxd[:, 0:192], T.ix[:], S16, None, OP.mult, None, [R("ix")], [R("pxd", 0, 192)])
+    ts(T.pxd[:, 192:384], T.idb[:], S16, None, OP.mult, None, [R("idb")], [R("pxd", 192, 384)])
+    tjrow = []
+
+    def to_row(q, tab, row, src, name, lo):
+        key = "%sr%d" % (tab, row)
+        dma(q, T[tab][row::16, :], src[:, lo:lo + 192], [R(name, lo, lo + 192), R(tab)], [R(key)])
+    to_row("S", "tj0", 0, T.j2, "j2", 0)
+    to_row("Y", "tj0", 1, T.pxd, "pxd", 0)
+    to_row("S", "tj0", 2, T.pxd, "pxd", 192)
     ts(T.nqi[:], T.nxb[:], 1.0 / 192, -95.5 / 192, OP.mult, OP.add, [R("nxb")], [R("nqi")])
     ts(T.nx2[:, 0:192], T.nqi[:], S16, None, OP.mult, None, [R("nqi")], [R("nx2", 0, 192)])
+    to_row("Y", "tj0", 3, T.nx2, "nx2", 0)
     ts(T.nt[:], T.nqi[:], -192.0, None, OP.mult, None, [R("nqi")], [R("nt")])
-    dma("S", T.tj0[2::16, :], T.nx2[:, 0:192], [R("nx2", 0, 192), R("tj0")], [R("tj0r2")])
     tt(T.nt2[:], T.nt[:], T.nxb[:], OP.add, [R("nxb"), R("nt")], [R("nt2")])
     ts(T.nx2[:, 192:384], T.nt2[:], S16, None, OP.mult, None, [R("nt2")], [R("nx2", 192, 384)])
-    dma("Y", T.tj0[3::16, :], T.nx2[:, 192:384], [R("nx2", 192, 384), R("tj0")], [R("tj0r3")])
-    TJ0 = [R("tj0"), R("tj0r0"), R("tj0r1"), R("tj0r2"), R("tj0r3")]
-    for j, v in ((I1, 1.0), (I1S, 65536.0), (I192, 192.0 * 65536), (I16, 16.0 * 65536), (ING, -BIG)):
-        ts(idm(j), T.im[:, 0:128], C(CP_), v, OP.is_equal, OP.mult, [R("im"), RC(CP_)], [R("ids", 128 * j, 128 * j + 128)])
-    ts(C(CGZ), C(CG), 15.0, None, OP.add, None, [RC(CG)], [RC(CGZ)])
-    ts(T.bo[:], T.igr[:], C(CG), None, OP.is_equal, None, [R("igr"), RC(CG)], [R("bo")])
-    ts(T.lb[:], T.im[:, 0:128], C(CG), None, OP.subtract, None, [R("im"), RC(CG)], [R("lb")])
-    ts(T.rst[:], T.kcb[:], 0.0, 1e9, OP.is_equal, OP.mult, [R("kcb")], [R("rst")])
+    to_row("Y", "tj0", 4, T.nx2, "nx2", 192)
+    TJ0 = [R("tj0")] + [R("tj0r%d" % r) for r in range(5)]
+    TJ1 = [R("tj1"), R("tj1r0"), R("tj1r2")]
+    dma("Y", T.thi[0::16, :], T.th[:], [], [R("thi")])
+    dma("Y", T.bmr[0::16, :], T.bm[:], [], [R("bmr")])
+    dma("Y", T.x15[:], T.xp[15::16, :], [], [R("x15")])
 
-    def col2(j, terms):
-        (r0, v0) = terms[0]
-        if len(terms) == 1:
-            ts(C(j), C(CR), float(r0), v0, OP.is_equal, OP.mult, [RC(CR)], [RC(j)])
-            return
-        (r1, v1) = terms[1]
-        ts(C(TA), C(CR), float(r0), v0, OP.is_equal, OP.mult, [RC(CR)], [RC(TA)])
-        ts(C(TB), C(CR), float(r1), v1, OP.is_equal, OP.mult, [RC(CR)], [RC(TB)])
-        tt(C(j), C(TA), C(TB), OP.add, [RC(TA), RC(TB)], [RC(j)])
-    u = 65536.0
-    ts(C(W0 + ZK), C(CR), 0.0, 16.0, OP.mult, OP.add, [RC(CR)], [RC(W0 + ZK)])
-    col2(W0 + ZQ, [(0, u)])
-    col2(W0 + ZN, [(1, u)])
-    col2(W0 + ZMA, [(2, 192 * u), (3, u)])
-    col2(W0 + ZMI, [(2, u), (3, 16 * u)])
-    col2(W0 + ZG, [(0, 512.0)])
-    col2(W0 + ZY, [(0, 192 * u), (1, u)])
-    for s in (ZK, ZQ, ZMA, ZN, ZG, ZMI, ZY):
-        ts(T.zs[:, 144 * s:144 * s + 144], T.im[:, 0:144], C(CGZ), C(W0 + s), OP.is_equal, OP.mult,
-           [R("im"), RC(CGZ), RC(W0 + s)], [R("zs", 144 * s, 144 * s + 144)])
-    Z = lambda s: R("zs", 144 * s, 144 * s + 144)
-    ID = lambda s: R("ids", 128 * s, 128 * s + 128)
-    ts(T.i0[:, 0:1], T.ria[:], 16, None, OP.mult, None, [R("ria")], [R("i0")])
-    cp(C(TA), T.i0[:, 0:1], [R("i0")], [RC(TA)])
-    ts(T.bs[:], T.bsi[:], C(TA), None, OP.add, None, [R("bsi"), RC(TA)], [R("bs")])
-    cp(T.k0[:], T.kti[:], [R("kti")], [R("k0")])
-
-    def make_hrep(h):
+    def make_hrep(h, sset, gset=()):
         for k in range(16):
             o, i = T.hrep[:, k::16], T[h][:]
-            if k % 3 != 2:
-                cp(o, i, [R(h)], [R("hrepv")] if k == 0 else [R("hrepv%d" % k)])
+            if k in gset:
+                op("G", lambda e: e.affine_select(o, i, [[0, 256]], OP.is_ge, 0.0, 1, 0), [R(h)], [R("hrep%d" % k)])
+            elif k not in sset:
+                cp(o, i, [R(h)], [R("hrep%d" % k)])
             else:
-                act(o, i, FN.Copy, [R(h)], [R("hreps%d" % k)])
-    HREP = [R("hrepv")] + [R("hrepv%d" % k) for k in range(1, 16) if k % 3 != 2] + [R("hreps%d" % k) for k in range(16) if k % 3 == 2]
-    make_hrep("h0")
+                act(o, i, FN.Copy, [R(h)], [R("hrep%d" % k)])
+    HREP = [R("hrep%d" % k) for k in range(16)]
+    make_hrep("h0", (0, 1, 2, 3, 5, 6, 7, 9, 10, 11, 13, 14), (4, 8, 12, 15))
+
+    tt(C(CG), C(CP_), C(CR), OP.subtract, [RC(CP_), RC(CR)], [RC(CG)])
+    ts(C(CGZ), C(CG), 15.0, None, OP.add, None, [RC(CG)], [RC(CGZ)])
+
+    def ident(j, v):
+        act(idm(j), idm(I1), FN.Copy, [R("ids", 0, 128)], [R("ids", 128 * j, 128 * j + 128)], scale=v)
+
+    def wcol(j, terms):
+        keys = []
+        for n, (r, v) in enumerate(terms):
+            dst = j if len(terms) == 1 else TA + n
+            ts(C(dst), C(CR), float(r), v, OP.is_equal, OP.mult, [RC(CR)], [RC(dst)])
+            keys.append(dst)
+        if len(keys) == 3:
+            tt(C(TA + 3), C(TA), C(TA + 1), OP.add, [RC(TA), RC(TA + 1)], [RC(TA + 3)])
+            tt(C(j), C(TA + 3), C(TA + 2), OP.add, [RC(TA + 3), RC(TA + 2)], [RC(j)])
+        elif len(keys) == 2:
+            tt(C(j), C(TA), C(TA + 1), OP.add, [RC(TA), RC(TA + 1)], [RC(j)])
+
+    def zset(s, terms):
+        if terms is None:
+            w, rd = 16.0, []
+        else:
+            if terms:
+                wcol(W0 + s, terms)
+            w, rd = C(W0 + s), [RC(W0 + s)]
+        act(T.zs[:, 144 * s:144 * s + 144], T.zb[:], FN.Copy, [R("zb")] + rd, [R("zs", 144 * s, 144 * s + 144)], scale=w)
+    ts(T.zb[:], T.im[:, 0:144], C(CGZ), None, OP.is_equal, None, [R("im"), RC(CGZ)], [R("zb")])
+    Z = lambda s: R("zs", 144 * s, 144 * s + 144)
+    ID = lambda s: R("ids", 128 * s, 128 * s + 128)
+    zset(ZK, None)
+    ts(T.bo[:], T.igr[:], C(CG), None, OP.is_equal, None, [R("igr"), RC(CG)], [R("bo")])
+    ts(T.rst[:], T.kcb[:], 0.0, 1e9, OP.is_equal, OP.mult, [R("kcb")], [R("rst")])
+    ts(T.r16[:], T.ria[:], 16, None, OP.mult, None, [R("ria")], [R("r16")])
+    cp(C(TA + 4), T.r16[:], [R("r16")], [RC(TA + 4)])
+    ts(T.bs[:], T.bsi[:], C(TA + 4), None, OP.add, None, [R("bsi"), RC(TA + 4)], [R("bs")])
+    cp(T.k0[:], T.kti[:], [R("kti")], [R("k0")])
+    zset(ZMA, [(3, 192 * U), (4, U)])
+
+
+    def setup_count():
+        wcol(WA, [(0, 4 * U), (1, U)])
+        wcol(WG, [(0, 1.0)])
+        wcol(WB, [(2, -U)])
+        wcol(W0 + ZQ, [(0, U)])
+        wcol(W0 + ZY, [(0, 192 * U), (1, 48 * U), (2, U)])
+        ts(T.rha[:], T.ig64[:], C(CG), C(WA), OP.is_equal, OP.mult, [R("ig64"), RC(CG), RC(WA)], [R("rha")])
+        ts(T.rhb[:], T.ig49[:], C(CG), C(WB), OP.is_equal, OP.mult, [R("ig49"), RC(CG), RC(WB)], [R("rhb")])
+        ts(T.cb[:], T.ig49[:], C(CG), C(WG), OP.is_equal, OP.mult, [R("ig49"), RC(CG), RC(WG)], [R("cb")])
+        ts(T.cbi[:], T.cbw[:], -0.5, None, OP.add, None, [R("cbw")], [R("cbi")])
+        tt(T.rhg[:], T.cb[:], T.cbi[:], OP.mult, [R("cb"), R("cbi")], [R("rhg")])
+    setup_count()
 
     for c in range(6):
         b = 2 + c
@@ -341,29 +294,52 @@ def rank_program(g, core, T, topo):
         else:
             cp(T.ev[:, sl], ps[b][:], [R("ps%d" % b)], [R("ev", 512 * c, 512 * c + 512)])
     dma("Y", T.plw[:], T.pl[:], [R("ev")], [R("plw")])
+    zset(ZQ, [])
+    zset(ZY, [])
 
-    def late_setup():
+    def setup_thr():
         ts(T.bof[:], T.igr[:], C(CG), None, OP.is_equal, None, [R("igr"), RC(CG)], [R("bof")])
         cp(T.thf[:], T.thi[:], [R("thi")], [R("thf")])
         mm(group(ps[4][:, 160:162], [(T.bof[:], T.thf[:])]), [R("bof"), R("thf")], [R("ps4", 160, 162)])
+        fill(T.zro[:], 0.0, "zro")
+        ident(ING, -BIG)
         ts(T.thr[:, 0:1], ps[4][:, 160:161], -0.5, None, OP.add, None, [R("ps4", 160, 162)], [R("thr", 0, 1)])
+        ts(T.thr[:, 2:3], ps[4][:, 160:161], -0.5, None, OP.add, None, [R("ps4", 160, 162)], [R("thr", 2, 3)])
         ts(T.thr[:, 1:2], ps[4][:, 161:162], 0.5 - BIG, None, OP.add, None, [R("ps4", 160, 162)], [R("thr", 1, 2)])
-        cp(T.thr[:, 2:3], T.thr[:, 0:1], [R("thr", 0, 1)], [R("thr", 2, 3)])
-        fill(T.n512[:], -512.0, "n512")
+
+    def setup_book():
         ts(T.bqi[:], T.bmr[:], 1.0 / 192, -95.5 / 192, OP.mult, OP.add, [R("bmr")], [R("bqi")])
         ts(T.bqs[:], T.bqi[:], S16, None, OP.mult, None, [R("bqi")], [R("bqs")])
         ts(T.bt[:], T.bqi[:], -192.0, None, OP.mult, None, [R("bqi")], [R("bt")])
         tt(T.bt2[:], T.bt[:], T.bmr[:], OP.add, [R("bt"), R("bmr")], [R("bt2")])
         ts(T.bns[:], T.bt2[:], S16, None, OP.mult, None, [R("bt2")], [R("bns")])
-        mm(group(ps[4][:, 96:112], wrapped(ZQ, T.bqs, 256)) + group(ps[4][:, 112:128], wrapped(ZQ, T.bns, 256)),
-           [R("bqs"), R("bns"), Z(ZQ)], [R("ps4", 96, 128)])
-        ts(T.mrow[:], T.igr[:], C(CG), C(W0 + ZMA), OP.is_equal, OP.mult, [R("igr"), RC(CG), RC(W0 + ZMA)], [R("mrow")])
+        mm(group(ps[4][:, 96:112], wrapped(ZY, T.bqs, 256) + wrapped(ZQ, T.bns, 256)),
+           [R("bqs"), R("bns"), Z(ZQ), Z(ZY)], [R("ps4", 96, 112)])
+
+    def setup_move():
+        ts(T.pk3[:], T.pci[:], 3, None, OP.bitwise_and, None, [R("pci")], [R("pk3")])
+        ts(T.pk4[:], T.pci[:], 2, None, OP.arith_shift_right, None, [R("pci")], [R("pk4")])
+        cp(C(KM), T.pk3[:], [R("pk3")], [RC(KM)])
+        ts(C(KD), T.pk4[:], 112.0, None, OP.add, None, [R("pk4")], [RC(KD)])
+        for x in range(4):
+            ts(C(WX + x), C(KM), float(x), VOID, OP.is_equal, OP.mult, [RC(KM)], [RC(WX + x)])
+            ts(T.zx[:, 240 * x:240 * x + 240], T.im[:], C(KD), C(WX + x), OP.is_equal, OP.mult,
+               [R("im"), RC(KD), RC(WX + x)], [R("zx")] if x == 0 else [R("zx%d" % x)])
+
+    def setup_state():
+        ts(T.j2[:, 192:384], T.ri[:], S16, None, OP.mult, None, [R("ri")], [R("j2", 192, 384)])
         tt(T.dd[:], T.nx2[:], T.j2[:], OP.subtract, [R("nx2"), R("j2")], [R("dd")])
         ts(T.d2[:], T.dd[:], 1.0 / VOID, None, OP.mult, None, [R("dd")], [R("d2")])
-        cp(T.v15[:], T.x15[:], [R("x15")], [R("v15")])
-        fill(T.tj1[:], 0.0, "tj1")
+        act(T.v15[:], T.x15[:], FN.Copy, [R("x15")], [R("v15")])
+        ident(I192, 192 * U)
+        ident(I1S, U)
+        ident(I16, 16 * U)
 
-    TJ1 = [R("tj1"), R("tj1r0"), R("tj1r1")]
+    def setup_last():
+        zset(ZMI, [(3, U), (4, 16 * U)])
+        zset(ZN, [(2, U)])
+        act(T.mrow[:], T.bo[:], FN.Copy, [R("bo"), RC(W0 + ZMA)], [R("mrow")], scale=C(W0 + ZMA))
+
     for hop in (1, 2):
         x = len(topo.engines(prv, core))
         arrive("ah%d" % hop, x, "hl%d" % hop, 256)
@@ -376,158 +352,188 @@ def rank_program(g, core, T, topo):
 
     def tj_piece(j):
         w = 24
+        if t == 0:
+            act(T.tj1[:, 384 * j:384 * j + 384], T.xsb[:, 384 * j:384 * j + 384], FN.Copy, [R("xsb")],
+                [R("tj1", 384 * j, 384 * j + 384)], scale=0.0)
+            return
         act(T.tj2[:, 16 * w * j:16 * w * (j + 1)], T.tj1[:, 0:P].indirect(T.jl[:, w * j:w * (j + 1)]), FN.Identity,
             TJ1 + [R("jl", w * j, w * (j + 1))], [R("tj2", 16 * w * j, 16 * w * (j + 1))])
+
+    def gen(u, ba, bb):
+        lo = 128 * u
+        sl = slice(lo, lo + 128)
+        mm(group(ps[ba][:], [(T.rs[:, sl], T.rha[:])]), [R("rs", lo, lo + 128), R("rha")], [R("ps%d" % ba)])
+        mm(group(ps[bb][:, 0:392], [(T.rs[:, sl], T.rhb[:]), (T.gob[:, sl], T.rhg[:])]),
+           [R("rs", lo, lo + 128), R("rhb"), R("gob", lo, lo + 128), R("rhg")], [R("ps%d" % bb)])
+
+    def isq(u, ba):
+        tt(T.oa[:, 512 * u:512 * u + 512], ps[ba][:], T.pat[:], OP.is_equal, [R("ps%d" % ba), R("pat")], [R("oa", u, u + 1)])
+
+    def sgn(u, bb):
+        act(T.sb[:, 392 * u:392 * u + 392], ps[bb][:, 0:392], FN.Sign, [R("ps%d" % bb)], [R("sb", u, u + 1)])
+
+    def prod(u):
+        mm([(ps[0][0:64, 49 * k:49 * k + 49], T.oa[:, 512 * u + 64 * k:512 * u + 64 * k + 64],
+             T.sb[:, 392 * u + 49 * k:392 * u + 49 * k + 49], False, u == 5 and k == 7) for k in range(8)],
+           [R("oa", u, u + 1), R("sb", u, u + 1)], [R("ps0")])
 
     for t in range(3):
         last = t == 2
         xt, xn = (T.ev, "ev") if t == 0 else (T.x2, "x2")
         kn = ("k0", "kl1", "kl2")[t]
         hn = ("h0", "hl1", "hl2")[t]
-        for c in range(4):
-            if t and c == 0:
-                tj_piece(0), tj_piece(1)
-            sl = slice(1024 * c, 1024 * c + 1024)
-            tt(T.dw[:, sl], xt[:, 0:P].indirect(T[kn][:, 64 * c:64 * c + 64]), T.hrep[:, sl], OP.subtract,
-               [R(xn), R(kn)] + HREP, [R("dw", 1024 * c, 1024 * c + 1024)])
-            for a in range(4 * c, 4 * c + 4, 4):
-                act(T.ab[:, a:a + 4, :], T.dw[:, sl], FN.Abs, [R("dw", 1024 * c, 1024 * c + 1024)],
-                    [R("ab", c, c + 1)])
-            mm(group(ps[0][:, 64 * c:64 * c + 64],
-                     [(idm(I1), T.kcb[:, 64 * c:64 * c + 64])] + [(z(ZK, r), T.ab[:, 4 * c:4 * c + 4, 16 * r:16 * r + 16]) for r in range(16)]),
-               [R("ab", c, c + 1), R("kcb"), Z(ZK), ID(I1)], [R("ps0", 64 * c, 64 * c + 64)])
-            if t:
-                tj_piece(2 + c)
+        tj_piece(0), tj_piece(1)
+        a0 = 0
+        for c, na in enumerate((5, 4, 4, 2, 1)):
+            a1 = a0 + na
+            lo, hi = 256 * a0, 256 * a1
+            tt(T.dw[:, lo:hi], xt[:, 0:P].indirect(T[kn][:, 16 * a0:16 * a1]), T.hrep[:, lo:hi], OP.subtract,
+               [R(xn), R(kn)] + HREP, [R("dw", lo, hi)])
+            act(T.ab[:, a0:a1, :], T.dw[:, lo:hi], FN.Abs, [R("dw", lo, hi)], [R("ab", a0, a1)])
+            mm(group(ps[0][:, 16 * a0:16 * a1],
+                     [(idm(I1), T.kcb[:, 16 * a0:16 * a1])] + [(z(ZK, r), T.ab[:, a0:a1, 16 * r:16 * r + 16]) for r in range(16)]),
+               [R("ab", a0, a1), R("kcb"), Z(ZK), ID(I1)], [R("ps0", 16 * a0, 16 * a1)])
+            a0 = a1
         if t == 0:
-            late_setup()
-        op("V", lambda e: e.tensor_tensor_scan(T.sc[:], T.rst[:], ps[0][:, 0:256], 1e9, OP.max, OP.min),
-           [R("rst"), R("ps0")], [R("sc")])
+            setup_thr()
+            setup_book()
+        tj_piece(2), tj_piece(3)
+        for lo, hi in ((0, 208), (208, 256)):
+            op("V", lambda e: e.tensor_tensor_scan(T.sc[:, lo:hi], T.rst[:, lo:hi], ps[0][:, lo:hi], 1e9, OP.max, OP.min),
+               [R("rst"), R("ps0", lo, hi)], [R("sc", lo, hi)])
         cp(T.i0[:], T.sc[:, 15::16], [R("sc")], [R("i0")])
         ts(T.i1[:], T.i0[:], 15, None, OP.bitwise_and, None, [R("i0")], [R("i1")])
         tt(T.i2[:], T.i1[:], T.bs[:], OP.add, [R("i1"), R("bs")], [R("i2")])
         cp(T.off[:], T.i2[:], [R("i2")], [R("off")])
         cp(T.w[:], T.dw[:, 0:4096].indirect(T.off[:]), [R("dw"), R("off")], [R("w")])
-        if t:
-            tj_piece(6), tj_piece(7)
         zm = ZMA if t == 0 else ZMI
-        qn_done = []
 
-        def digits(lo, hi, go_lo):
-            n = 16 * (hi - lo)
-            base = 32 * lo
-            mm(group(ps[4][:, base:base + n],
-                     [(idm(I1), T.n512[:, 0:n])] + wrapped(ZQ, T.rs, 256 * hi, 256 * lo) + wrapped(ZG, T.gob, 256 * hi, 256 * lo))
-               + group(ps[4][:, base + n:base + 2 * n], wrapped(ZN, T.rs, 256 * hi, 256 * lo)),
-               [R("rs", 256 * lo, 256 * hi), R("gob", 256 * lo, 256 * hi), R("n512"), ID(I1), Z(ZQ), Z(ZG), Z(ZN)],
-               [R("ps4", base, base + 2 * n)])
-            cp(T.qn[:, base:base + 2 * n], ps[4][:, base:base + 2 * n], [R("ps4", base, base + 2 * n)], [R("qn", base, base + 2 * n)])
-            ts(T.nb[:, 16 * lo:16 * hi], T.qn[:, base + n:base + 2 * n], -1.0, 0.5, OP.mult, OP.add,
-               [R("qn", base, base + 2 * n)], [R("nb", 16 * lo, 16 * hi)])
-            return base, base + n
+        def places(s0, s1):
+            lo, hi = 256 * s0, 256 * s1
+            b, w = 32 * s0, 16 * (s1 - s0)
+            mm(group(ps[4][:, b:b + w], wrapped(ZY, T.rs, hi, lo)) + group(ps[4][:, b + w:b + 2 * w], wrapped(ZG, T.gob, hi, lo)),
+               [R("rs", lo, hi), R("gob", lo, hi), Z(ZY), Z(ZG)], [R("ps4", b, b + 2 * w)])
 
-        first = {"V": True, "S": True}
-        stops = {"V": 32 + 8, "S": 47}
+        def listed(s0, s1):
+            b, w = 32 * s0, 16 * (s1 - s0)
+            cp(T.yg[:, b:b + w], ps[4][:, b:b + w], [R("ps4", b, b + 2 * w)], [R("yg", b, b + w)])
+            ts(T.yg[:, b + w:b + 2 * w], ps[4][:, b + w:b + 2 * w], S16, None, OP.mult, None, [R("ps4", b, b + 2 * w)],
+               [R("yg", b + w, b + 2 * w)])
 
-        def count(items, qcol, ncol, s_items):
-            for j, it in enumerate(items):
-                lsl = slice(128 * it, 128 * it + 128)
-                ts(T.lh[:, lsl], T.lb[:], T.qn[:, qcol + j:qcol + j + 1], None, OP.is_equal, None,
-                   [R("lb"), R("qn", qcol, qcol + len(items))], [R("lh", 128 * it, 128 * it + 128)])
-                if it in s_items:
-                    rsl = slice(208 * it, 208 * it + 193)
-                    act(T.rh[:, rsl], T.rix[:], FN.Sign, [R("rix"), R("nb", it, it + 1)], [R("rh", 208 * it, 208 * it + 208)],
-                        bias=T.nb[:, it:it + 1])
-                    out, key, rg = ps[0][:, 0:193], "S", "ps0"
-                else:
-                    rsl = slice(208 * it, 208 * it + 192)
-                    ts(T.rh[:, rsl], T.ri[:], T.qn[:, ncol + j:ncol + j + 1], None, OP.is_equal, None,
-                       [R("ri"), R("qn", ncol, ncol + len(items))], [R("rh", 208 * it, 208 * it + 208)])
-                    out, key, rg = ps[5][:, 0:192], "V", "ps5"
-                mm([(out, T.lh[:, lsl], T.rh[:, rsl], first[key], it == last_item[key])],
-                   [R("lh", 128 * it, 128 * it + 128), R("rh", 208 * it, 208 * it + 208)], [R(rg)])
-                first[key] = False
-        s_set = set(range(2, 32, 5)) | set(range(0, 32, 5)) | set(range(33, 48, 5)) | set(range(35, 48, 5))
-        last_item = {"S": max(s_set), "V": max(i for i in range(48) if i not in s_set)}
+        def pick(s):
+            y, c = 16 * s, 48 + 16 * s
+            y0, y1 = "yy%d" % s, "yy%d" % (s + 1)
+            k = slice(16 * s, 16 * s + 16)
+            kr = lambda n: R(n, 16 * s, 16 * s + 16)
+            tt(T.ta[:, k], T.yg[:, y:y + 16], T[y0][:], OP.subtract, [R("yg", y, y + 16), R(y0)], [kr("ta")])
+            tt(T.tb[:, k], T.ta[:, k], T.yg[:, c:c + 16], OP.mult, [kr("ta"), R("yg", c, c + 16)], [kr("tb")])
+            tt(T[y1][:], T[y0][:], T.tb[:, k], OP.add, [kr("tb"), R(y0)], [R(y1)])
 
-        def pick(lo, qcol, ncol):
-            qs, ns = T.qn[:, qcol:qcol + 16], T.qn[:, ncol:ncol + 16]
-            rq = [R("qn", qcol, qcol + 16), R("qn", ncol, ncol + 16)]
-            ts(T.gw[:, 0:16], qs, -0.5, None, OP.is_ge, None, rq, [R("gw", 0, 16)])
-            tt(T.t32[:, 0:16], qs, T.yy[:, 0:16], OP.subtract, rq + [R("yy", 0, 16)], [R("t32", 0, 16)])
-            tt(T.t32[:, 16:32], ns, T.yy[:, 16:32], OP.subtract, rq + [R("yy", 16, 32)], [R("t32", 16, 32)])
-            tt(T.t32[:, 0:16], T.t32[:, 0:16], T.gw[:, 0:16], OP.mult, [R("t32", 0, 16), R("gw", 0, 16)], [R("t32", 0, 16)])
-            tt(T.t32[:, 16:32], T.t32[:, 16:32], T.gw[:, 0:16], OP.mult, [R("t32", 16, 32), R("gw", 0, 16)], [R("t32", 16, 32)])
-            tt(T.yy[:], T.yy[:], T.t32[:], OP.add, [R("t32"), R("yy")], [R("yy")])
+        jwrap = [(ps[3][:, lo:lo + 192], z(zz, r), T.tj2[:, r::16], r == 0, r == 15)
+                 for lo, zz in ((128, ZQ), (320, ZN)) for r in range(16)]
+
+        def jpart(j):
+            if t:
+                mm(jwrap[8 * j:8 * j + 8], [R("tj2"), Z(ZQ), Z(ZN)], [R("ps3", 128, 512)])
 
         for s in range(3):
-            c0 = 256 * s
-            rsl = slice(c0, c0 + 256)
-            hin = (hn, "hx0", "hx1")[s]
-            hout = ("hx0", "hx1", "hs%d" % t)[s]
+            c0, c1 = 256 * s, 256 * s + 256
+            rsl = slice(c0, c1)
+            hin = (hn, "hi0", "hi1")[s]
+            hout = ("hi0", "hi1", "hs%d" % t)[s]
             act(T.a1[:], T.w[:], FN.Abs, [R("w")], [R("a1")])
-            if s:
+            if s < 2:
+                act(T.hv[:], T.w[:], FN.Identity, [R("w")], [R("hv")], bias=-0.25, scale=0.5)
+            if s == 0:
+                mm([(ps[0][0:64, 0:392], T.ids[:, 0:64], T.zro[:], True, False)], [ID(I1), R("zro")], [R("ps0")])
+            else:
                 mm([(ps[1][:, 0:256], idm(ING), T.gob[:, c0 - 256:c0], True, False)], [R("gob", c0 - 256, c0), ID(ING)], [R("ps1")])
             ts(ps[6][:, 0:256], T.w[:], MAGIC, MAGIC, OP.add, OP.subtract, [R("w")], [R("ps6", 0, 256)])
-            tt(T.rs[:, rsl], T.w[:], ps[6][:, 0:256], OP.subtract, [R("w"), R("ps6", 0, 256)], [R("rs", c0, c0 + 256)])
+            tt(T.rs[:, rsl], T.w[:], ps[6][:, 0:256], OP.subtract, [R("w"), R("ps6", 0, 256)], [R("rs", c0, c1)])
             mm([(ps[1][:, 0:256], T.bo[:], T.a1[:], s == 0, True)], [R("a1"), R("bo")], [R("ps1")])
             if s < 2:
-                mm(group(ps[3][:, 0:16], wrapped(zm, T.rs, c0 + 256, c0)), [R("rs", c0, c0 + 256), Z(zm)], [R("ps3")])
-            ts(T.qb[:], T.w[:], 0.5, -0.25, OP.mult, OP.add, [R("w")], [R("qb")])
+                mm(group(ps[4][:, 192:208], wrapped(zm, T.rs, c1, c0)), [R("rs", c0, c1), Z(zm)], [R("ps4", 192, 208)])
+            else:
+                ts(T.qb[:], T.w[:], 0.5, -0.25, OP.mult, OP.add, [R("w")], [R("qb")])
+            qq, qn = (T.hv, "hv") if s < 2 else (T.qb, "qb")
+            if s:
+                isq(2 * s - 2, 5)
+                sgn(2 * s - 2, 7)
+                tj_piece(5 + s)
             th = T.thr[:, 2:3] if s == 0 else T.thr[:, 1:2]
             ts(ps[2][:, 0:256], ps[1][:, 0:256], th, None, OP.is_le, None, [R("ps1"), R("thr", 1, 3)], [R("ps2", 0, 256)])
-            tt(ps[2][:, 256:512], T.qb[:], ps[2][:, 0:256], OP.mult, [R("qb"), R("ps2", 0, 256)], [R("ps2", 256, 512)])
+            tt(ps[2][:, 256:512], qq[:], ps[2][:, 0:256], OP.mult, [R(qn), R("ps2", 0, 256)], [R("ps2", 256, 512)])
             tt(T[hout][:], T[hin][:], ps[2][:, 256:512], OP.add, [R(hin), R("ps2", 256, 512)], [R(hout)])
             if s < 2:
-                cp(T.ml[:], ps[3][:, 0:16], [R("ps3")], [R("ml")])
+                cp(T.ml[:], ps[4][:, 192:208], [R("ps4", 192, 208)], [R("ml")])
             if s == 0:
-                act(T.gob[:, rsl], ps[2][:, 0:256], FN.Copy, [R("ps2", 0, 256)], [R("gob", c0, c0 + 256), R("acn")], accum_out=T.acn[:])
+                act(T.gob[:, rsl], ps[2][:, 0:256], FN.Copy, [R("ps2", 0, 256)], [R("gob", c0, c1), R("acn")], accum_out=T.acn[:])
             else:
-                act(T.gob[:, rsl], ps[2][:, 0:256], FN.Copy, [R("ps2", 0, 256)], [R("gob", c0, c0 + 256)])
+                act(T.gob[:, rsl], ps[2][:, 0:256], FN.Copy, [R("ps2", 0, 256)], [R("gob", c0, c1)])
             if s < 2:
                 tt(T.w[:], xt[:, 0:P].indirect(T.ml[:]), T[hout][:], OP.subtract, [R(xn), R("ml"), R(hout)], [R("w")])
-            if s == 1:
-                qa, na = digits(0, 2, 0)
+            if s:
+                if s == 2:
+                    jpart(0)
+                gen(2 * s - 1, 5, 7)
+                prod(2 * s - 2)
+                isq(2 * s - 1, 5)
+                sgn(2 * s - 1, 7)
+            gen(2 * s, 5, 7)
+            if s < 2:
+                tj_piece(4 + s)
+            if s:
+                prod(2 * s - 1)
+            if t and s == 2:
+                act(T.rb[:], T.tj2[:, 0:P].indirect(T.bl[:]), FN.Identity, [R("tj2"), R("bl")], [R("rb")])
+        gen(5, 1, 6)
         if not last:
             send("hl%d" % (t + 1), "hs%d" % t, "ah%d" % (t + 1))
         else:
             dma("Y", T.yh[:], T.hs2[:], [R("hs2")], [R("yh")])
+        isq(4, 5)
+        sgn(4, 7)
+        jpart(1)
+        prod(4)
+        isq(5, 1)
+        sgn(5, 6)
+        jpart(2)
+        prod(5)
+        jpart(3)
+        if t == 0:
+            setup_move()
+            setup_state()
+            setup_last()
+        act(T.sgc[0:64, 0:392], ps[0][0:64, 0:392], FN.Copy, [R("ps0")], [R("sgc")])
+        tt(T.flg[0:64, 0:391], ps[0][0:64, 1:392], T.sgc[0:64, 0:391], OP.is_gt, [R("ps0"), R("sgc")], [R("flg")])
+        for x in range(4):
+            mm(group(ps[5][:, 48 * x:48 * x + 48], [(T.zx[0:64, 240 * x + 112 - 16 * k:240 * x + 240 - 16 * k],
+                                                     T.flg[0:64, 49 * k:49 * k + 48]) for k in range(8)]),
+               [R("flg"), R("zx")] + [R("zx%d" % i) for i in (1, 2, 3)], [R("ps5", 48 * x, 48 * x + 48)])
         if t:
-            act(T.rb[:], T.tj2[:, 0:P].indirect(T.bl[:]), FN.Identity, [R("tj2"), R("bl")], [R("rb")])
-            mm(group(ps[4][:, 96:112], wrapped(ZQ, T.rb, 256)) + group(ps[4][:, 112:128], wrapped(ZN, T.rb, 256)),
-               [R("rb"), Z(ZQ), Z(ZN)], [R("ps4", 96, 128)])
-            mm(group(ps[7][:, 0:192], [(z(ZQ, r), T.tj2[:, r::16]) for r in range(16)])
-               + group(ps[7][:, 192:384], [(z(ZN, r), T.tj2[:, r::16]) for r in range(16)]),
-               [R("tj2"), Z(ZQ), Z(ZN)], [R("ps7")])
-        count(list(range(32)), qa, na, s_set)
-        qc, nc = digits(2, 3, 0)
-        count(list(range(32, 48)), qc, nc, s_set)
-        if t:
-            ts(T.j2[:], ps[7][:, 0:384], S16, None, OP.mult, None, [R("ps7")], [R("j2")])
+            ts(T.j2[:], ps[3][:, 128:512], S16, None, OP.mult, None, [R("ps3", 128, 512)], [R("j2")])
             tt(T.dd[:], T.nx2[:], T.j2[:], OP.subtract, [R("nx2"), R("j2")], [R("dd")])
             ts(T.d2[:], T.dd[:], 1.0 / VOID, None, OP.mult, None, [R("dd")], [R("d2")])
-        act(T.sgc[:, 0:192], ps[0][:, 0:192], FN.Copy, [R("ps0")], [R("sgc")])
-        tt(T.dfc[:], ps[0][:, 1:193], T.sgc[:, 0:192], OP.subtract, [R("ps0"), R("sgc")], [R("dfc")])
-        tt(T.cnt[:], T.dfc[:], ps[5][:, 0:192], OP.add, [R("dfc"), R("ps5")], [R("cnt")])
-        ts(ps[6][:, 0:192], T.cnt[:], 0.5, VOID, OP.is_gt, OP.mult, [R("cnt")], [R("ps6", 0, 192)])
+            mm(group(ps[4][:, 96:112], wrapped(ZY, T.rb, 256)), [R("rb"), Z(ZY)], [R("ps4", 96, 112)])
+        places(0, 3)
         if not last:
-            tt(T.v15[:], T.v15[:], ps[6][:, 0:192], OP.add, [R("v15"), R("ps6", 0, 192)], [R("v15")])
+            tt(T.v15[:], T.v15[:], ps[5][:, 0:192], OP.add, [R("v15"), R("ps5")], [R("v15")])
             dma("Y", T.ev[15::16, :], T.v15[:], [R("v15")], [R("ev")])
-        ts(ps[6][:, 192:384], T.cnt[:], 0.5, VOID, OP.is_gt, OP.mult, [R("cnt")], [R("ps6", 192, 384)])
-        tt(ps[2][:, 0:384], T.d2[:], ps[6][:, 0:384], OP.mult, [R("d2"), R("ps6", 0, 384)], [R("ps2", 0, 384)])
+        tt(ps[2][:, 0:192], T.d2[:, 0:192], ps[5][:, 0:192], OP.mult, [R("d2"), R("ps5")], [R("ps2", 0, 192)])
+        tt(ps[2][:, 192:384], T.d2[:, 192:384], ps[5][:, 0:192], OP.mult, [R("d2"), R("ps5")], [R("ps2", 192, 384)])
         tt(T.j2n[:], T.j2[:], ps[2][:, 0:384], OP.add, [R("j2"), R("ps2", 0, 384)], [R("j2n")])
-        dma("Y", T.tj1[0::16, :], T.j2n[:, 0:192], [R("j2n"), R("tj1")], [R("tj1r0")])
-        dma("Y", T.tj1[1::16, :], T.j2n[:, 192:384], [R("j2n"), R("tj1")], [R("tj1r1")])
-        mm(group(ps[7][:, 0:192], [(idm(I192), T.j2n[:, 0:192]), (idm(I1S), T.j2n[:, 192:384])])
-           + group(ps[7][:, 192:384], [(idm(I1S), T.j2n[:, 0:192]), (idm(I16), T.j2n[:, 192:384])]),
-           [R("j2n"), ID(I192), ID(I1S), ID(I16)], [R("ps7")])
-        cp(T.jl[:], ps[7][:, 0:384], [R("ps7")], [R("jl")])
-        cp(T.yy[:], ps[4][:, 96:128], [R("ps4", 96, 128)], [R("yy")])
-        pick(0, qa, na)
-        pick(1, qa + 16, na + 16)
-        pick(2, qc, nc)
-        ts(T.y1[:], T.yy[:, 0:16], 192.0, None, OP.mult, None, [R("yy")], [R("y1")])
-        tt(T.y2[:], T.y1[:], T.yy[:, 16:32], OP.add, [R("y1"), R("yy")], [R("y2")])
-        cp(T.yl[:], T.y2[:], [R("y2")], [R("yl")])
+        to_row("Y", "tj1", 0, T.j2n, "j2n", 0)
+        to_row("Y", "tj1", 2, T.j2n, "j2n", 192)
+        mm(group(ps[3][:, 128:320], [(idm(I192), T.j2n[:, 0:192]), (idm(I1S), T.j2n[:, 192:384])])
+           + group(ps[3][:, 320:512], [(idm(I1S), T.j2n[:, 0:192]), (idm(I16), T.j2n[:, 192:384])]),
+           [R("j2n"), ID(I192), ID(I1S), ID(I16)], [R("ps3", 128, 512)])
+        cp(T.yy0[:], ps[4][:, 96:112], [R("ps4", 96, 112)], [R("yy0")])
+        listed(0, 3)
+        pick(0)
+        cp(T.jl[:], ps[3][:, 128:512], [R("ps3", 128, 512)], [R("jl")])
+        pick(1)
+        pick(2)
+        cp(T.yl[:], T.yy3[:], [R("yy3")], [R("yl")])
         act(T.ry[:], T.tj0[:, 0:P].indirect(T.yl[:]), FN.Identity, TJ0 + [R("yl")], [R("ry")])
         if not last:
             ts(T.g16[:], T.plw[:, 0:P].indirect(T.yl[:]), 16.0, None, OP.mult, None, [R("plw"), R("yl")], [R("g16")])
@@ -537,16 +543,19 @@ def rank_program(g, core, T, topo):
             cp(T["ks%d" % t][:], T.kk[:], [R("kk")], [R("ks%d" % t)])
             send("kl%d" % (t + 1), "ks%d" % t, "ak%d" % (t + 1))
             mm(group(ps[4][:, 128:144], wrapped(ZMI, T.ry, 256)), [R("ry"), Z(ZMI)], [R("ps4", 128, 144)])
-            cp(T.bl[:], ps[4][:, 128:144], [R("ps4", 128, 144)], [R("bl")])
+            make_hrep("hl%d" % (t + 1), (2, 5, 8, 11, 14), (1, 6, 12, 15))
+
+            def through(src, sn, dst, dn, lo, nv):
+                op("V", lambda e: e.tensor_copy(dst[:, 0:16 * nv], src[:, 0:P].indirect(T.jl[:, lo:lo + nv])),
+                   [R(sn), R("jl", lo, lo + nv)], [R(dn, 0, 16 * nv)])
+                act(dst[:, 16 * nv:3072], src[:, 0:P].indirect(T.jl[:, lo + nv:lo + 192]), FN.Identity,
+                    [R(sn), R("jl", lo + nv, lo + 192)], [R(dn, 16 * nv, 3072)])
+            through(T.ev, "ev", T.x1, "x1", 0, 80)
             cp(T.aci[:], T.acn[:], [R("acn")], [R("aci")])
             ts(T.acj[:], T.aci[:], 31, None, OP.bitwise_and, None, [R("aci")], [R("acj")])
             tt(T.thr[:, 2:3], T.acj[:], T.thr[:, 0:1], OP.add, [R("acj"), R("thr", 0, 1)], [R("thr", 2, 3)])
-            make_hrep("hl%d" % (t + 1))
-            for src, sn, dst, dn, lo in ((T.ev, "ev", T.x1, "x1", 0), (T.x1, "x1", T.x2, "x2", 192)):
-                op("V", lambda e: e.tensor_copy(dst[:, 0:1536], src[:, 0:P].indirect(T.jl[:, lo:lo + 96])),
-                   [R(sn), R("jl", lo, lo + 96)], [R(dn, 0, 1536)])
-                act(dst[:, 1536:3072], src[:, 0:P].indirect(T.jl[:, lo + 96:lo + 192]), FN.Identity,
-                    [R(sn), R("jl", lo + 96, lo + 192)], [R(dn, 1536, 3072)])
+            cp(T.bl[:], ps[4][:, 128:144], [R("ps4", 128, 144)], [R("bl")])
+            through(T.x1, "x1", T.x2, "x2", 192, 96)
         else:
             mm(group(ps[1][:, 0:256], [(T.mrow[:], T.ry[:])]), [R("mrow"), R("ry")], [R("ps1")])
             act(T.ybs[:], ps[1][:, 0:256], FN.Copy, [R("ps1")], [R("ybs")])

@@ -18,10 +18,10 @@ def _sb(dtype, **names):
 
 
 _sb("bfloat16", xsb=P, tj0=P, tj1=P, tj2=P, ab=(16, 256), hrep=4096, oa=6 * 512, sb=6 * 392, h0=256, hl1=256, hl2=256,
-    hx0=256, hx1=256, hs0=256, hs1=256, hs2=256, a1=256, rs=768, gob=768, rb=256, ry=256, x15=192, nx2=384, j2=384,
+    hx0=256, hx1=256, hs0=256, hs1=256, hs2=256, a1=256, rs=768, gob=768, rb=256, ry=256, x15=192, nx2=384, nxu=384, j2=384,
     j2n=384, pxd=384, bqs=256, bns=256, flg=400, ri=192, im=240, igr=128, ig64=512, ig49=392, kcb=256, zs=6 * 144, zb=144,
     ids=5 * 128, bo=128, mrow=128, rha=512, rhg=392, rhb=392, cbi=392, cbw=392, cb=392, pat=512, zro=392, zx=4 * 240, ix=192, idb=192)
-_sb("float32", ev=P, x1=P, x2=P, dw=4096, sc=256, w=256, yg=96, yy0=16, yy1=16, yy2=16, yy3=16, ta=48, tb=48, g16=256,
+_sb("float32", ev=P, x1=P, x2=P, dw=4096, sc=256, w=256, yg=112, yy1=16, yy2=16, yy3=16, ta=48, tb=48, g16=256,
     kk=256, sgc=400, v15=192, nt=192, nt2=192, dd=384, d2=384, bt=256, bt2=256, thf=2, thr=8, acn=1, ybs=256, yjs=192,
     hv=256, cols=40, bof=128, rst=256)
 _sb("int32", hi0=256, hi1=256, plw=P, kti=256, i0=16, i1=16, i2=16, qb=256, kq=256, nxb=192, nqi=192, bmr=256, bqi=256, thi=2, aci=1, acj=1,
@@ -220,8 +220,8 @@ def rank_program(g, core, T, topo):
     dma("Y", T.bmr[0::16, :], T.bm[:], [], [R("bmr")])
     dma("Y", T.x15[:], T.xp[15::16, :], [], [R("x15")])
 
-    def make_hrep(h, sset, gset=()):
-        for k in range(16):
+    def make_hrep(h, sset, gset=(), ks=range(16)):
+        for k in ks:
             o, i = T.hrep[:, k::16], T[h][:]
             if k in gset:
                 op("G", lambda e: e.affine_select(o, i, [[0, 256]], OP.is_ge, 0.0, 1, 0), [R(h)], [R("hrep%d" % k)])
@@ -303,6 +303,12 @@ def rank_program(g, core, T, topo):
         mm(group(ps[4][:, 160:162], [(T.bof[:], T.thf[:])]), [R("bof"), R("thf")], [R("ps4", 160, 162)])
         fill(T.zro[:], 0.0, "zro")
         ident(ING, -BIG)
+        act(T.v15[:], T.x15[:], FN.Copy, [R("x15")], [R("v15")])
+        ident(I192, 192 * U)
+        ident(I1S, U)
+        ident(I16, 16 * U)
+
+    def setup_thr2():
         ts(T.thr[:, 0:1], ps[4][:, 160:161], -0.5, None, OP.add, None, [R("ps4", 160, 162)], [R("thr", 0, 1)])
         ts(T.thr[:, 2:3], ps[4][:, 160:161], -0.5, None, OP.add, None, [R("ps4", 160, 162)], [R("thr", 2, 3)])
         ts(T.thr[:, 1:2], ps[4][:, 161:162], 0.5 - BIG, None, OP.add, None, [R("ps4", 160, 162)], [R("thr", 1, 2)])
@@ -311,10 +317,12 @@ def rank_program(g, core, T, topo):
         ts(T.bqi[:], T.bmr[:], 1.0 / 192, -95.5 / 192, OP.mult, OP.add, [R("bmr")], [R("bqi")])
         ts(T.bqs[:], T.bqi[:], S16, None, OP.mult, None, [R("bqi")], [R("bqs")])
         ts(T.bt[:], T.bqi[:], -192.0, None, OP.mult, None, [R("bqi")], [R("bt")])
+
+    def setup_book2():
         tt(T.bt2[:], T.bt[:], T.bmr[:], OP.add, [R("bt"), R("bmr")], [R("bt2")])
         ts(T.bns[:], T.bt2[:], S16, None, OP.mult, None, [R("bt2")], [R("bns")])
-        mm(group(ps[4][:, 96:112], wrapped(ZY, T.bqs, 256) + wrapped(ZQ, T.bns, 256)),
-           [R("bqs"), R("bns"), Z(ZQ), Z(ZY)], [R("ps4", 96, 112)])
+        mm(group(ps[4][:, 0:16], wrapped(ZY, T.bqs, 256) + wrapped(ZQ, T.bns, 256)),
+           [R("bqs"), R("bns"), Z(ZQ), Z(ZY)], [R("ps4", 0, 16)])
 
     def setup_move():
         ts(T.pk3[:], T.pci[:], 3, None, OP.bitwise_and, None, [R("pci")], [R("pk3")])
@@ -329,15 +337,12 @@ def rank_program(g, core, T, topo):
     def setup_state():
         ts(T.j2[:, 192:384], T.ri[:], S16, None, OP.mult, None, [R("ri")], [R("j2", 192, 384)])
         tt(T.dd[:], T.nx2[:], T.j2[:], OP.subtract, [R("nx2"), R("j2")], [R("dd")])
-        ts(T.d2[:], T.dd[:], 1.0 / VOID, None, OP.mult, None, [R("dd")], [R("d2")])
-        act(T.v15[:], T.x15[:], FN.Copy, [R("x15")], [R("v15")])
-        ident(I192, 192 * U)
-        ident(I1S, U)
-        ident(I16, 16 * U)
+        act(T.d2[:], T.dd[:], FN.Copy, [R("dd")], [R("d2")], scale=1.0 / VOID)
 
     def setup_last():
-        zset(ZMI, [(3, U), (4, 16 * U)])
-        zset(ZN, [(2, U)])
+        act(T.nxu[:], T.nx2[:], FN.Copy, [R("nx2")], [R("nxu")], scale=U)
+        zset(ZMI, [])
+        zset(ZN, [])
         act(T.mrow[:], T.bo[:], FN.Copy, [R("bo"), RC(W0 + ZMA)], [R("mrow")], scale=C(W0 + ZMA))
 
     for hop in (1, 2):
@@ -362,7 +367,10 @@ def rank_program(g, core, T, topo):
     def gen(u, ba, bb):
         lo = 128 * u
         sl = slice(lo, lo + 128)
-        mm(group(ps[ba][:], [(T.rs[:, sl], T.rha[:])]), [R("rs", lo, lo + 128), R("rha")], [R("ps%d" % ba)])
+        if ba is not None:
+            mm(group(ps[ba][:], [(T.rs[:, sl], T.rha[:])]), [R("rs", lo, lo + 128), R("rha")], [R("ps%d" % ba)])
+        if bb is None:
+            return
         mm(group(ps[bb][:, 0:392], [(T.rs[:, sl], T.rhb[:]), (T.gob[:, sl], T.rhg[:])]),
            [R("rs", lo, lo + 128), R("rhb"), R("gob", lo, lo + 128), R("rhg")], [R("ps%d" % bb)])
 
@@ -397,6 +405,11 @@ def rank_program(g, core, T, topo):
         if t == 0:
             setup_thr()
             setup_book()
+        else:
+            cp(T.aci[:], T.acn[:], [R("acn")], [R("aci")])
+            ts(T.acj[:], T.aci[:], 31, None, OP.bitwise_and, None, [R("aci")], [R("acj")])
+            tt(T.thr[:, 2:3], T.acj[:], T.thr[:, 0:1], OP.add, [R("acj"), R("thr", 0, 1)], [R("thr", 2, 3)])
+            cp(T.bl[:], ps[4][:, 128:144], [R("ps4", 128, 144)], [R("bl")])
         tj_piece(2), tj_piece(3)
         for lo, hi in ((0, 208), (208, 256)):
             op("V", lambda e: e.tensor_tensor_scan(T.sc[:, lo:hi], T.rst[:, lo:hi], ps[0][:, lo:hi], 1e9, OP.max, OP.min),
@@ -408,26 +421,18 @@ def rank_program(g, core, T, topo):
         cp(T.w[:], T.dw[:, 0:4096].indirect(T.off[:]), [R("dw"), R("off")], [R("w")])
         zm = ZMA if t == 0 else ZMI
 
-        def places(s0, s1):
-            lo, hi = 256 * s0, 256 * s1
-            b, w = 32 * s0, 16 * (s1 - s0)
-            mm(group(ps[4][:, b:b + w], wrapped(ZY, T.rs, hi, lo)) + group(ps[4][:, b + w:b + 2 * w], wrapped(ZG, T.gob, hi, lo)),
-               [R("rs", lo, hi), R("gob", lo, hi), Z(ZY), Z(ZG)], [R("ps4", b, b + 2 * w)])
+        def places():
+            mm(group(ps[4][:, 16:64], wrapped(ZY, T.rs, 768)) + group(ps[4][:, 64:112], wrapped(ZG, T.gob, 768)),
+               [R("rs"), R("gob"), Z(ZY), Z(ZG)], [R("ps4", 16, 112)])
 
-        def listed(s0, s1):
-            b, w = 32 * s0, 16 * (s1 - s0)
-            cp(T.yg[:, b:b + w], ps[4][:, b:b + w], [R("ps4", b, b + 2 * w)], [R("yg", b, b + w)])
-            ts(T.yg[:, b + w:b + 2 * w], ps[4][:, b + w:b + 2 * w], S16, None, OP.mult, None, [R("ps4", b, b + 2 * w)],
-               [R("yg", b + w, b + 2 * w)])
-
-        def pick(s):
-            y, c = 16 * s, 48 + 16 * s
-            y0, y1 = "yy%d" % s, "yy%d" % (s + 1)
-            k = slice(16 * s, 16 * s + 16)
-            kr = lambda n: R(n, 16 * s, 16 * s + 16)
-            tt(T.ta[:, k], T.yg[:, y:y + 16], T[y0][:], OP.subtract, [R("yg", y, y + 16), R(y0)], [kr("ta")])
-            tt(T.tb[:, k], T.ta[:, k], T.yg[:, c:c + 16], OP.mult, [kr("ta"), R("yg", c, c + 16)], [kr("tb")])
-            tt(T[y1][:], T[y0][:], T.tb[:, k], OP.add, [kr("tb"), R(y0)], [R(y1)])
+        def pick():
+            ts(T.yg[:], ps[4][:, 0:112], S16, None, OP.mult, None, [R("ps4", 0, 112)], [R("yg")])
+            tt(T.ta[:], T.yg[:, 16:64], T.yg[:, 0:48], OP.subtract, [R("yg")], [R("ta")])
+            tt(T.tb[:], T.ta[:], T.yg[:, 64:112], OP.mult, [R("ta"), R("yg")], [R("tb")])
+            tt(T.yy1[:], T.tb[:, 0:16], T.yg[:, 0:16], OP.add, [R("tb"), R("yg")], [R("yy1")])
+            tt(T.yy2[:], T.tb[:, 16:32], T.tb[:, 32:48], OP.add, [R("tb")], [R("yy2")])
+            tt(T.yy3[:], T.yy1[:], T.yy2[:], OP.add, [R("yy1"), R("yy2")], [R("yy3")])
+            ts(T.yl[:], T.yy3[:], U, None, OP.mult, None, [R("yy3")], [R("yl")])
 
         jwrap = [(ps[3][:, lo:lo + 192], z(zz, r), T.tj2[:, r::16], r == 0, r == 15)
                  for lo, zz in ((128, ZQ), (320, ZN)) for r in range(16)]
@@ -455,6 +460,8 @@ def rank_program(g, core, T, topo):
                 mm(group(ps[4][:, 192:208], wrapped(zm, T.rs, c1, c0)), [R("rs", c0, c1), Z(zm)], [R("ps4", 192, 208)])
             else:
                 ts(T.qb[:], T.w[:], 0.5, -0.25, OP.mult, OP.add, [R("w")], [R("qb")])
+            if t == 0 and s == 0:
+                setup_thr2()
             qq, qn = (T.hv, "hv") if s < 2 else (T.qb, "qb")
             if s:
                 isq(2 * s - 2, 5)
@@ -473,9 +480,10 @@ def rank_program(g, core, T, topo):
             if s < 2:
                 tt(T.w[:], xt[:, 0:P].indirect(T.ml[:]), T[hout][:], OP.subtract, [R(xn), R("ml"), R(hout)], [R("w")])
             if s:
-                if s == 2:
-                    jpart(0)
                 gen(2 * s - 1, 5, 7)
+                if s == 2:
+                    gen(5, 6, None)
+                    jpart(0)
                 prod(2 * s - 2)
                 isq(2 * s - 1, 5)
                 sgn(2 * s - 1, 7)
@@ -484,26 +492,22 @@ def rank_program(g, core, T, topo):
                 tj_piece(4 + s)
             if s:
                 prod(2 * s - 1)
-            if t and s == 2:
-                act(T.rb[:], T.tj2[:, 0:P].indirect(T.bl[:]), FN.Identity, [R("tj2"), R("bl")], [R("rb")])
-        gen(5, 1, 6)
+        gen(5, None, 1)
         if not last:
             send("hl%d" % (t + 1), "hs%d" % t, "ah%d" % (t + 1))
         else:
             dma("Y", T.yh[:], T.hs2[:], [R("hs2")], [R("yh")])
+        isq(5, 6)
         isq(4, 5)
         sgn(4, 7)
         jpart(1)
         prod(4)
-        isq(5, 1)
-        sgn(5, 6)
-        jpart(2)
+        sgn(5, 1)
         prod(5)
+        jpart(2)
         jpart(3)
         if t == 0:
             setup_move()
-            setup_state()
-            setup_last()
         act(T.sgc[0:64, 0:392], ps[0][0:64, 0:392], FN.Copy, [R("ps0")], [R("sgc")])
         tt(T.flg[0:64, 0:391], ps[0][0:64, 1:392], T.sgc[0:64, 0:391], OP.is_gt, [R("ps0"), R("sgc")], [R("flg")])
         for x in range(4):
@@ -511,11 +515,15 @@ def rank_program(g, core, T, topo):
                                                      T.flg[0:64, 49 * k:49 * k + 48]) for k in range(8)]),
                [R("flg"), R("zx")] + [R("zx%d" % i) for i in (1, 2, 3)], [R("ps5", 48 * x, 48 * x + 48)])
         if t:
-            ts(T.j2[:], ps[3][:, 128:512], S16, None, OP.mult, None, [R("ps3", 128, 512)], [R("j2")])
-            tt(T.dd[:], T.nx2[:], T.j2[:], OP.subtract, [R("nx2"), R("j2")], [R("dd")])
-            ts(T.d2[:], T.dd[:], 1.0 / VOID, None, OP.mult, None, [R("dd")], [R("d2")])
-            mm(group(ps[4][:, 96:112], wrapped(ZY, T.rb, 256)), [R("rb"), Z(ZY)], [R("ps4", 96, 112)])
-        places(0, 3)
+            tt(T.dd[:], T.nxu[:], ps[3][:, 128:512], OP.subtract, [R("nxu"), R("ps3", 128, 512)], [R("dd")])
+            act(T.rb[:], T.tj2[:, 0:P].indirect(T.bl[:]), FN.Identity, [R("tj2"), R("bl")], [R("rb")])
+            act(T.j2[:], ps[3][:, 128:512], FN.Copy, [R("ps3", 128, 512)], [R("j2")], scale=S16)
+            act(T.d2[:], T.dd[:], FN.Copy, [R("dd")], [R("d2")], scale=S16 / VOID)
+            mm(group(ps[4][:, 0:16], wrapped(ZY, T.rb, 256)), [R("rb"), Z(ZY)], [R("ps4", 0, 16)])
+        else:
+            setup_state()
+            setup_book2()
+        places()
         if not last:
             tt(T.v15[:], T.v15[:], ps[5][:, 0:192], OP.add, [R("v15"), R("ps5")], [R("v15")])
             dma("Y", T.ev[15::16, :], T.v15[:], [R("v15")], [R("ev")])
@@ -527,36 +535,37 @@ def rank_program(g, core, T, topo):
         mm(group(ps[3][:, 128:320], [(idm(I192), T.j2n[:, 0:192]), (idm(I1S), T.j2n[:, 192:384])])
            + group(ps[3][:, 320:512], [(idm(I1S), T.j2n[:, 0:192]), (idm(I16), T.j2n[:, 192:384])]),
            [R("j2n"), ID(I192), ID(I1S), ID(I16)], [R("ps3", 128, 512)])
-        cp(T.yy0[:], ps[4][:, 96:112], [R("ps4", 96, 112)], [R("yy0")])
-        listed(0, 3)
-        pick(0)
+        if t == 0:
+            wcol(W0 + ZMI, [(3, U), (4, 16 * U)])
+            wcol(W0 + ZN, [(2, U)])
         cp(T.jl[:], ps[3][:, 128:512], [R("ps3", 128, 512)], [R("jl")])
-        pick(1)
-        pick(2)
-        cp(T.yl[:], T.yy3[:], [R("yy3")], [R("yl")])
-        act(T.ry[:], T.tj0[:, 0:P].indirect(T.yl[:]), FN.Identity, TJ0 + [R("yl")], [R("ry")])
+        pick()
+
+        def book():
+            act(T.ry[:], T.tj0[:, 0:P].indirect(T.yl[:]), FN.Identity, TJ0 + [R("yl")], [R("ry")])
         if not last:
+            make_hrep("hl%d" % (t + 1), (2, 4, 7, 10, 12, 15), (0, 3, 6, 9, 13), (0, 2, 3, 4, 6, 7, 9, 10, 12, 13, 15))
             ts(T.g16[:], T.plw[:, 0:P].indirect(T.yl[:]), 16.0, None, OP.mult, None, [R("plw"), R("yl")], [R("g16")])
             ts(T.kq[:], T.g16[:], 1.0 / 3072, -1528.0 / 3072, OP.mult, OP.add, [R("g16")], [R("kq")])
             ts(ps[6][:, 0:256], T.kq[:], -3071.0, None, OP.mult, None, [R("kq")], [R("ps6", 0, 256)])
             tt(T.kk[:], T.g16[:], ps[6][:, 0:256], OP.add, [R("g16"), R("ps6", 0, 256)], [R("kk")])
             cp(T["ks%d" % t][:], T.kk[:], [R("kk")], [R("ks%d" % t)])
             send("kl%d" % (t + 1), "ks%d" % t, "ak%d" % (t + 1))
-            mm(group(ps[4][:, 128:144], wrapped(ZMI, T.ry, 256)), [R("ry"), Z(ZMI)], [R("ps4", 128, 144)])
-            make_hrep("hl%d" % (t + 1), (2, 5, 8, 11, 14), (1, 6, 12, 15))
+            make_hrep("hl%d" % (t + 1), (), (1, 5, 8, 11, 14), (1, 5, 8, 11, 14))
 
             def through(src, sn, dst, dn, lo, nv):
                 op("V", lambda e: e.tensor_copy(dst[:, 0:16 * nv], src[:, 0:P].indirect(T.jl[:, lo:lo + nv])),
                    [R(sn), R("jl", lo, lo + nv)], [R(dn, 0, 16 * nv)])
                 act(dst[:, 16 * nv:3072], src[:, 0:P].indirect(T.jl[:, lo + nv:lo + 192]), FN.Identity,
                     [R(sn), R("jl", lo + nv, lo + 192)], [R(dn, 16 * nv, 3072)])
-            through(T.ev, "ev", T.x1, "x1", 0, 80)
-            cp(T.aci[:], T.acn[:], [R("acn")], [R("aci")])
-            ts(T.acj[:], T.aci[:], 31, None, OP.bitwise_and, None, [R("aci")], [R("acj")])
-            tt(T.thr[:, 2:3], T.acj[:], T.thr[:, 0:1], OP.add, [R("acj"), R("thr", 0, 1)], [R("thr", 2, 3)])
-            cp(T.bl[:], ps[4][:, 128:144], [R("ps4", 128, 144)], [R("bl")])
+            through(T.ev, "ev", T.x1, "x1", 0, 60)
             through(T.x1, "x1", T.x2, "x2", 192, 96)
+            if t == 0:
+                setup_last()
+            book()
+            mm(group(ps[4][:, 128:144], wrapped(ZMI, T.ry, 256)), [R("ry"), Z(ZMI)], [R("ps4", 128, 144)])
         else:
+            book()
             mm(group(ps[1][:, 0:256], [(T.mrow[:], T.ry[:])]), [R("mrow"), R("ry")], [R("ps1")])
             act(T.ybs[:], ps[1][:, 0:256], FN.Copy, [R("ps1")], [R("ybs")])
             dma("Y", T.yb[:], T.ybs[0::16, :], [R("ybs")], [R("yb")])

@@ -20,7 +20,7 @@ def _sb(dtype, **names):
 _sb("bfloat16", xsb=P, tj0=P, tj1=P, tj2=P, ab=(16, 256), hrep=4096, oa=6 * 512, sb=6 * 392, h0=256, hl1=256, hl2=256,
     hx0=256, hx1=256, hs0=256, hs1=256, hs2=256, a1=256, rs=768, gob=768, rb=256, ry=256, x15=192, nx2=384, nxu=384, j2=384,
     j2n=384, pxd=384, bqs=256, bns=256, flg=400, ri=192, im=240, igr=128, ig64=512, ig49=392, kcb=256, zs=6 * 144, zb=144,
-    ids=5 * 128, bo=128, mrow=128, rha=512, rhg=392, rhb=392, cbi=392, cbw=392, cb=392, pat=512, zro=392, zx=4 * 240, ix=192, idb=192)
+    ids=5 * 128, bo=128, mrow=128, rha=512, rhg=392, rhb=392, cbi=392, cbw=392, pat=512, zro=392, zx=4 * 240, ix=192, idb=192)
 _sb("float32", ev=P, x1=P, x2=P, dw=4096, sc=256, w=256, yg=112, yy1=16, yy2=16, yy3=16, ta=48, tb=48, g16=256,
     kk=256, sgc=400, v15=192, nt=192, nt2=192, dd=384, d2=384, bt=256, bt2=256, thf=2, thr=8, acn=1, ybs=256, yjs=192,
     hv=256, cols=40, bof=128, rst=256)
@@ -279,9 +279,9 @@ def rank_program(g, core, T, topo):
         wcol(W0 + ZY, [(0, 192 * U), (1, 48 * U), (2, U)])
         ts(T.rha[:], T.ig64[:], C(CG), C(WA), OP.is_equal, OP.mult, [R("ig64"), RC(CG), RC(WA)], [R("rha")])
         ts(T.rhb[:], T.ig49[:], C(CG), C(WB), OP.is_equal, OP.mult, [R("ig49"), RC(CG), RC(WB)], [R("rhb")])
-        ts(T.cb[:], T.ig49[:], C(CG), C(WG), OP.is_equal, OP.mult, [R("ig49"), RC(CG), RC(WG)], [R("cb")])
-        ts(T.cbi[:], T.cbw[:], -0.5, None, OP.add, None, [R("cbw")], [R("cbi")])
-        tt(T.rhg[:], T.cb[:], T.cbi[:], OP.mult, [R("cb"), R("cbi")], [R("rhg")])
+        act(T.cbi[:], T.cbw[:], FN.Identity, [R("cbw")], [R("cbi")], bias=-0.5)
+        ts(ps[0][:, 0:392], T.ig49[:], C(CG), C(WG), OP.is_equal, OP.mult, [R("ig49"), RC(CG), RC(WG)], [R("ps0")])
+        tt(T.rhg[:], T.cbi[:], ps[0][:, 0:392], OP.mult, [R("ps0"), R("cbi")], [R("rhg")])
     setup_count()
 
     for c in range(6):
@@ -289,7 +289,7 @@ def rank_program(g, core, T, topo):
         sl = slice(512 * c, 512 * c + 512)
         mm(group(ps[b][:], [(idm(I1), T.xsb[:, sl]), (idm(I1), T.tj0[:, sl])]),
            [ID(I1), R("xsb", 512 * c, 512 * c + 512)] + TJ0, [R("ps%d" % b)])
-        if c % 2:
+        if c not in (3, 5):
             act(T.ev[:, sl], ps[b][:], FN.Copy, [R("ps%d" % b)], [R("ev", 512 * c, 512 * c + 512)])
         else:
             cp(T.ev[:, sl], ps[b][:], [R("ps%d" % b)], [R("ev", 512 * c, 512 * c + 512)])
@@ -341,9 +341,10 @@ def rank_program(g, core, T, topo):
 
     def setup_last():
         act(T.nxu[:], T.nx2[:], FN.Copy, [R("nx2")], [R("nxu")], scale=U)
-        zset(ZMI, [])
-        zset(ZN, [])
         act(T.mrow[:], T.bo[:], FN.Copy, [R("bo"), RC(W0 + ZMA)], [R("mrow")], scale=C(W0 + ZMA))
+
+    def book():
+        act(T.ry[:], T.tj0[:, 0:P].indirect(T.yl[:]), FN.Identity, TJ0 + [R("yl")], [R("ry")])
 
     for hop in (1, 2):
         x = len(topo.engines(prv, core))
@@ -390,6 +391,8 @@ def rank_program(g, core, T, topo):
         xt, xn = (T.ev, "ev") if t == 0 else (T.x2, "x2")
         kn = ("k0", "kl1", "kl2")[t]
         hn = ("h0", "hl1", "hl2")[t]
+        if t:
+            book()
         tj_piece(0), tj_piece(1)
         a0 = 0
         for c, na in enumerate((5, 4, 4, 2, 1)):
@@ -398,9 +401,10 @@ def rank_program(g, core, T, topo):
             tt(T.dw[:, lo:hi], xt[:, 0:P].indirect(T[kn][:, 16 * a0:16 * a1]), T.hrep[:, lo:hi], OP.subtract,
                [R(xn), R(kn)] + HREP, [R("dw", lo, hi)])
             act(T.ab[:, a0:a1, :], T.dw[:, lo:hi], FN.Abs, [R("dw", lo, hi)], [R("ab", a0, a1)])
-            mm(group(ps[0][:, 16 * a0:16 * a1],
+            kb, klo = (0, 16 * a0) if a1 < 16 else (1, 0)
+            mm(group(ps[kb][:, klo:klo + 16 * na],
                      [(idm(I1), T.kcb[:, 16 * a0:16 * a1])] + [(z(ZK, r), T.ab[:, a0:a1, 16 * r:16 * r + 16]) for r in range(16)]),
-               [R("ab", a0, a1), R("kcb"), Z(ZK), ID(I1)], [R("ps0", 16 * a0, 16 * a1)])
+               [R("ab", a0, a1), R("kcb"), Z(ZK), ID(I1)], [R("ps%d" % kb, klo, klo + 16 * na)])
             a0 = a1
         if t == 0:
             setup_thr()
@@ -409,11 +413,10 @@ def rank_program(g, core, T, topo):
             cp(T.aci[:], T.acn[:], [R("acn")], [R("aci")])
             ts(T.acj[:], T.aci[:], 31, None, OP.bitwise_and, None, [R("aci")], [R("acj")])
             tt(T.thr[:, 2:3], T.acj[:], T.thr[:, 0:1], OP.add, [R("acj"), R("thr", 0, 1)], [R("thr", 2, 3)])
-            cp(T.bl[:], ps[4][:, 128:144], [R("ps4", 128, 144)], [R("bl")])
         tj_piece(2), tj_piece(3)
-        for lo, hi in ((0, 208), (208, 256)):
-            op("V", lambda e: e.tensor_tensor_scan(T.sc[:, lo:hi], T.rst[:, lo:hi], ps[0][:, lo:hi], 1e9, OP.max, OP.min),
-               [R("rst"), R("ps0", lo, hi)], [R("sc", lo, hi)])
+        for kb, lo, hi in ((0, 0, 240), (1, 240, 256)):
+            op("V", lambda e: e.tensor_tensor_scan(T.sc[:, lo:hi], T.rst[:, lo:hi], ps[kb][:, lo * (1 - kb):lo * (1 - kb) + hi - lo],
+                                                   1e9, OP.max, OP.min), [R("rst"), R("ps%d" % kb, 0, 240)], [R("sc", lo, hi)])
         cp(T.i0[:], T.sc[:, 15::16], [R("sc")], [R("i0")])
         ts(T.i1[:], T.i0[:], 15, None, OP.bitwise_and, None, [R("i0")], [R("i1")])
         tt(T.i2[:], T.i1[:], T.bs[:], OP.add, [R("i1"), R("bs")], [R("i2")])
@@ -434,12 +437,12 @@ def rank_program(g, core, T, topo):
             tt(T.yy3[:], T.yy1[:], T.yy2[:], OP.add, [R("yy1"), R("yy2")], [R("yy3")])
             ts(T.yl[:], T.yy3[:], U, None, OP.mult, None, [R("yy3")], [R("yl")])
 
-        jwrap = [(ps[3][:, lo:lo + 192], z(zz, r), T.tj2[:, r::16], r == 0, r == 15)
-                 for lo, zz in ((128, ZQ), (320, ZN)) for r in range(16)]
-
         def jpart(j):
+            lo = 96 * (j // 2)
             if t:
-                mm(jwrap[8 * j:8 * j + 8], [R("tj2"), Z(ZQ), Z(ZN)], [R("ps3", 128, 512)])
+                mm(group(ps[3][:, 128 + lo + 192 * (j % 2):224 + lo + 192 * (j % 2)],
+                         [(z((ZQ, ZN)[j % 2], r), T.tj2[:, 16 * lo + r:16 * lo + 1536:16]) for r in range(16)]),
+                   [R("tj2", 16 * lo, 16 * lo + 1536), Z(ZQ), Z(ZN)], [R("ps3", 128, 512)])
 
         for s in range(3):
             c0, c1 = 256 * s, 256 * s + 256
@@ -453,11 +456,15 @@ def rank_program(g, core, T, topo):
                 mm([(ps[0][0:64, 0:392], T.ids[:, 0:64], T.zro[:], True, False)], [ID(I1), R("zro")], [R("ps0")])
             else:
                 mm([(ps[1][:, 0:256], idm(ING), T.gob[:, c0 - 256:c0], True, False)], [R("gob", c0 - 256, c0), ID(ING)], [R("ps1")])
-            ts(ps[6][:, 0:256], T.w[:], MAGIC, MAGIC, OP.add, OP.subtract, [R("w")], [R("ps6", 0, 256)])
-            tt(T.rs[:, rsl], T.w[:], ps[6][:, 0:256], OP.subtract, [R("w"), R("ps6", 0, 256)], [R("rs", c0, c1)])
+            if t or s == 0:
+                ts(ps[6][:, 0:256], T.w[:], MAGIC, MAGIC, OP.add, OP.subtract, [R("w")], [R("ps6", 0, 256)])
+                tt(T.rs[:, rsl], T.w[:], ps[6][:, 0:256], OP.subtract, [R("w"), R("ps6", 0, 256)], [R("rs", c0, c1)])
             mm([(ps[1][:, 0:256], T.bo[:], T.a1[:], s == 0, True)], [R("a1"), R("bo")], [R("ps1")])
             if s < 2:
                 mm(group(ps[4][:, 192:208], wrapped(zm, T.rs, c1, c0)), [R("rs", c0, c1), Z(zm)], [R("ps4", 192, 208)])
+                if t and s == 0:
+                    mm(group(ps[4][:, 128:144], wrapped(ZMI, T.ry, 256)), [R("ry"), Z(ZMI)], [R("ps4", 128, 144)])
+                    jpart(0)
             else:
                 ts(T.qb[:], T.w[:], 0.5, -0.25, OP.mult, OP.add, [R("w")], [R("qb")])
             if t == 0 and s == 0:
@@ -466,7 +473,11 @@ def rank_program(g, core, T, topo):
             if s:
                 isq(2 * s - 2, 5)
                 sgn(2 * s - 2, 7)
-                tj_piece(5 + s)
+            if t == 0 and s == 2:
+                setup_last()
+            tj_piece(4 + s)
+            if s == 2:
+                tj_piece(7)
             th = T.thr[:, 2:3] if s == 0 else T.thr[:, 1:2]
             ts(ps[2][:, 0:256], ps[1][:, 0:256], th, None, OP.is_le, None, [R("ps1"), R("thr", 1, 3)], [R("ps2", 0, 256)])
             tt(ps[2][:, 256:512], qq[:], ps[2][:, 0:256], OP.mult, [R(qn), R("ps2", 0, 256)], [R("ps2", 256, 512)])
@@ -477,19 +488,23 @@ def rank_program(g, core, T, topo):
                 act(T.gob[:, rsl], ps[2][:, 0:256], FN.Copy, [R("ps2", 0, 256)], [R("gob", c0, c1), R("acn")], accum_out=T.acn[:])
             else:
                 act(T.gob[:, rsl], ps[2][:, 0:256], FN.Copy, [R("ps2", 0, 256)], [R("gob", c0, c1)])
+            if t == 0 and s < 2:
+                act(T.rs[:, c1:c1 + 256], T.tj0[:, 0:P].indirect(T.ml[:]), FN.Identity, TJ0 + [R("ml")], [R("rs", c1, c1 + 256)])
             if s < 2:
                 tt(T.w[:], xt[:, 0:P].indirect(T.ml[:]), T[hout][:], OP.subtract, [R(xn), R("ml"), R(hout)], [R("w")])
+            if s == 1:
+                jpart(1)
             if s:
                 gen(2 * s - 1, 5, 7)
                 if s == 2:
                     gen(5, 6, None)
-                    jpart(0)
+                    jpart(2)
                 prod(2 * s - 2)
                 isq(2 * s - 1, 5)
                 sgn(2 * s - 1, 7)
             gen(2 * s, 5, 7)
-            if s < 2:
-                tj_piece(4 + s)
+            if t and s == 1:
+                cp(T.bl[:], ps[4][:, 128:144], [R("ps4", 128, 144)], [R("bl")])
             if s:
                 prod(2 * s - 1)
         gen(5, None, 1)
@@ -500,13 +515,12 @@ def rank_program(g, core, T, topo):
         isq(5, 6)
         isq(4, 5)
         sgn(4, 7)
-        jpart(1)
         prod(4)
         sgn(5, 1)
         prod(5)
-        jpart(2)
         jpart(3)
         if t == 0:
+            setup_book2()
             setup_move()
         act(T.sgc[0:64, 0:392], ps[0][0:64, 0:392], FN.Copy, [R("ps0")], [R("sgc")])
         tt(T.flg[0:64, 0:391], ps[0][0:64, 1:392], T.sgc[0:64, 0:391], OP.is_gt, [R("ps0"), R("sgc")], [R("flg")])
@@ -516,13 +530,12 @@ def rank_program(g, core, T, topo):
                [R("flg"), R("zx")] + [R("zx%d" % i) for i in (1, 2, 3)], [R("ps5", 48 * x, 48 * x + 48)])
         if t:
             tt(T.dd[:], T.nxu[:], ps[3][:, 128:512], OP.subtract, [R("nxu"), R("ps3", 128, 512)], [R("dd")])
-            act(T.rb[:], T.tj2[:, 0:P].indirect(T.bl[:]), FN.Identity, [R("tj2"), R("bl")], [R("rb")])
-            act(T.j2[:], ps[3][:, 128:512], FN.Copy, [R("ps3", 128, 512)], [R("j2")], scale=S16)
             act(T.d2[:], T.dd[:], FN.Copy, [R("dd")], [R("d2")], scale=S16 / VOID)
-            mm(group(ps[4][:, 0:16], wrapped(ZY, T.rb, 256)), [R("rb"), Z(ZY)], [R("ps4", 0, 16)])
+            act(T.j2[:], ps[3][:, 128:512], FN.Copy, [R("ps3", 128, 512)], [R("j2")], scale=S16)
+            act(T.rb[:], T.tj2[:, 0:P].indirect(T.bl[:]), FN.Identity, [R("tj2"), R("bl")], [R("rb")])
+
         else:
             setup_state()
-            setup_book2()
         places()
         if not last:
             tt(T.v15[:], T.v15[:], ps[5][:, 0:192], OP.add, [R("v15"), R("ps5")], [R("v15")])
@@ -535,23 +548,25 @@ def rank_program(g, core, T, topo):
         mm(group(ps[3][:, 128:320], [(idm(I192), T.j2n[:, 0:192]), (idm(I1S), T.j2n[:, 192:384])])
            + group(ps[3][:, 320:512], [(idm(I1S), T.j2n[:, 0:192]), (idm(I16), T.j2n[:, 192:384])]),
            [R("j2n"), ID(I192), ID(I1S), ID(I16)], [R("ps3", 128, 512)])
+        if t:
+            mm(group(ps[4][:, 0:16], wrapped(ZY, T.rb, 256)), [R("rb"), Z(ZY)], [R("ps4", 0, 16)])
         if t == 0:
             wcol(W0 + ZMI, [(3, U), (4, 16 * U)])
             wcol(W0 + ZN, [(2, U)])
         cp(T.jl[:], ps[3][:, 128:512], [R("ps3", 128, 512)], [R("jl")])
         pick()
-
-        def book():
-            act(T.ry[:], T.tj0[:, 0:P].indirect(T.yl[:]), FN.Identity, TJ0 + [R("yl")], [R("ry")])
         if not last:
-            make_hrep("hl%d" % (t + 1), (2, 4, 7, 10, 12, 15), (0, 3, 6, 9, 13), (0, 2, 3, 4, 6, 7, 9, 10, 12, 13, 15))
+            make_hrep("hl%d" % (t + 1), (2, 4, 7, 10, 12, 14), (0, 3, 6, 9, 13), (0, 2, 3, 4, 6, 7, 9, 10, 12, 13, 14))
+            if t == 0:
+                zset(ZMI, [])
+                zset(ZN, [])
             ts(T.g16[:], T.plw[:, 0:P].indirect(T.yl[:]), 16.0, None, OP.mult, None, [R("plw"), R("yl")], [R("g16")])
             ts(T.kq[:], T.g16[:], 1.0 / 3072, -1528.0 / 3072, OP.mult, OP.add, [R("g16")], [R("kq")])
             ts(ps[6][:, 0:256], T.kq[:], -3071.0, None, OP.mult, None, [R("kq")], [R("ps6", 0, 256)])
             tt(T.kk[:], T.g16[:], ps[6][:, 0:256], OP.add, [R("g16"), R("ps6", 0, 256)], [R("kk")])
             cp(T["ks%d" % t][:], T.kk[:], [R("kk")], [R("ks%d" % t)])
             send("kl%d" % (t + 1), "ks%d" % t, "ak%d" % (t + 1))
-            make_hrep("hl%d" % (t + 1), (), (1, 5, 8, 11, 14), (1, 5, 8, 11, 14))
+            make_hrep("hl%d" % (t + 1), (), (1, 5, 8, 11, 15), (1, 5, 8, 11, 15))
 
             def through(src, sn, dst, dn, lo, nv):
                 op("V", lambda e: e.tensor_copy(dst[:, 0:16 * nv], src[:, 0:P].indirect(T.jl[:, lo:lo + nv])),
@@ -560,20 +575,21 @@ def rank_program(g, core, T, topo):
                     [R(sn), R("jl", lo + nv, lo + 192)], [R(dn, 16 * nv, 3072)])
             through(T.ev, "ev", T.x1, "x1", 0, 60)
             through(T.x1, "x1", T.x2, "x2", 192, 96)
-            if t == 0:
-                setup_last()
-            book()
-            mm(group(ps[4][:, 128:144], wrapped(ZMI, T.ry, 256)), [R("ry"), Z(ZMI)], [R("ps4", 128, 144)])
+
         else:
+            for lo in (0, 48):
+                b = lo + 96
+                cp(T.tj2[:, 16 * lo:16 * lo + 768], T.tj1[:, 0:P].indirect(T.jl[:, lo:lo + 48]),
+                   TJ1 + [R("jl", lo, lo + 48)], [R("tj2", 16 * lo, 16 * lo + 768)])
+                act(T.tj2[:, 16 * b:16 * b + 768], T.tj1[:, 0:P].indirect(T.jl[:, b:b + 48]), FN.Identity,
+                    TJ1 + [R("jl", b, b + 48)], [R("tj2", 16 * b, 16 * b + 768)])
+                for c in (lo, b):
+                    mm(group(ps[7][:, c:c + 48], [(z(ZY, r), T.tj2[:, 16 * c + r:16 * c + 768:16]) for r in range(16)]),
+                       [R("tj2", 16 * c, 16 * c + 768), Z(ZY)], [R("ps7", c, c + 48)])
+            cp(T.yjs[:], ps[7][:, 0:192], [R("ps7")], [R("yjs")])
+            dma("Y", T.yj[:], T.yjs[:], [R("yjs")], [R("yj")])
             book()
             mm(group(ps[1][:, 0:256], [(T.mrow[:], T.ry[:])]), [R("mrow"), R("ry")], [R("ps1")])
             act(T.ybs[:], ps[1][:, 0:256], FN.Copy, [R("ps1")], [R("ybs")])
-            dma("Y", T.yb[:], T.ybs[0::16, :], [R("ybs")], [R("yb")])
-            op("V", lambda e: e.tensor_copy(T.tj2[:, 0:1536], T.tj1[:, 0:P].indirect(T.jl[:, 0:96])),
-               TJ1 + [R("jl", 0, 96)], [R("tj2", 0, 1536)])
-            act(T.tj2[:, 1536:3072], T.tj1[:, 0:P].indirect(T.jl[:, 96:192]), FN.Identity,
-                TJ1 + [R("jl", 96, 192)], [R("tj2", 1536, 3072)])
-            mm(group(ps[7][:, 0:192], [(z(ZY, r), T.tj2[:, r::16]) for r in range(16)]), [R("tj2"), Z(ZY)], [R("ps7")])
-            cp(T.yjs[:], ps[7][:, 0:192], [R("ps7")], [R("yjs")])
-            dma("Y", T.yj[:], T.yjs[:], [R("yjs")], [R("yj")])
+            dma("S", T.yb[:], T.ybs[0::16, :], [R("ybs")], [R("yb")])
     finish()

from concourse.mybir import dt, AluOpType, AxisListType, ActivationFunctionType

OP = AluOpType
FN = ActivationFunctionType
P, L = 3072, 256
S16 = 2.0 ** -16
U = 65536.0
BIG = 16384.0
VOID = 8192.0
MAGIC = 12582912.0

SCRATCH = {}


def _sb(dtype, **names):
    for name, cols in names.items():
        SCRATCH[name] = ("sbuf", [128] + (list(cols) if isinstance(cols, tuple) else [cols]), dtype)


_sb("bfloat16", xsb=P, tj0=P, tj1=P, tj2=P, ab=(16, 256), hrep=4096, oa=6 * 512, sb=6 * 392, h0=256, hl1=256, hl2=256,
    hx0=256, hx1=256, hs0=256, hs1=256, hs2=256, a1=256, rs=768, gob=768, rb=256, ry=256, x15=192, nx2=384, nxu=384, j2=384,
    j2n=384, pxd=384, bqs=256, bns=256, flg=400, ri=192, im=240, igr=128, ig64=512, ig49=392, kcb=256, zs=6 * 144, zb=144,
    ids=5 * 128, bo=128, mrow=128, rha=512, rhg=392, rhb=392, cbi=392, cbw=392, pat=512, zro=392, zx=4 * 240, ix=192, idb=192)
_sb("float32", ev=P, x1=P, x2=P, dw=4096, sc=256, w=256, yg=112, yy1=16, yy2=16, yy3=16, ta=48, tb=48, g16=256,
    kk=256, sgc=400, v15=192, nt=192, nt2=192, dd=384, d2=384, bt=256, bt2=256, thf=2, thr=8, acn=1, ybs=256, yjs=192,
    hv=256, cols=40, bof=128, rst=256)
_sb("int32", hi0=256, hi1=256, plw=P, kti=256, i0=16, i1=16, i2=16, qb=256, kq=256, nxb=192, nqi=192, bmr=256, bqi=256, thi=2, aci=1, acj=1,
    pci=1, ria=1, pk3=1, pk4=1, bsi=16, bs=16, r16=1)
_sb("uint16", k0=256, ks0=256, ks1=256, kl1=256, kl2=256, off=16, ml=16, yl=16, bl=16, jl=384)
for _b in range(8):
    SCRATCH["ps%d" % _b] = ("psum", [128, 512], "float32")
SEMAPHORES = ["sV", "sS", "sP", "sG", "ls", "ah1", "ak1", "ah2", "ak2"] + ["d%d" % _i for _i in range(40)]

ZK, ZQ, ZN, ZMA, ZMI, ZY = range(6)
ZG = ZQ
I1, I192, I1S, I16, ING = range(5)


def make(g, T):
    eng = {"V": g.vector, "S": g.scalar, "P": g.tensor, "G": g, "Y": g.sync}
    total, known, clock, hist, waited = {}, {q: {} for q in eng}, {}, {}, {}

    def need(q, deps):
        for sem, val in sorted(deps, key=lambda d: -d[1]):
            if known[q].get(sem, 0) >= val:
                continue
            eng[q].wait_ge(T.sem[sem], val)
            waited[sem] = max(waited.get(sem, 0), val)
            for s, v in clock[(sem, val)].items():
                if known[q].get(s, 0) < v:
                    known[q][s] = v

    def conflicts(q, reads, writes, noself):
        deps = {}
        for accs, wr in ((reads, False), (writes, True)):
            for name, lo, hi in accs:
                ps = name[:2] == "ps"
                for (tok, eq, ew, elo, ehi) in hist.get(name, []):
                    over = lo < ehi and elo < hi
                    if eq == q and tok[0][0] == "s":
                        c = over and (ew or wr) and not (noself and wr)
                    else:
                        c = (over and (ew or wr)) or (ps and eq != q)
                    if c:
                        deps[tok[0]] = max(deps.get(tok[0], 0), tok[1])
        return list(deps.items())

    def record(tok, q, reads, writes):
        for accs, wr in ((reads, False), (writes, True)):
            for name, lo, hi in accs:
                hs = hist.setdefault(name, [])
                if wr:
                    hs[:] = [e for e in hs if not (lo <= e[3] and e[4] <= hi)]
                else:
                    hs[:] = [e for e in hs if not (e[0][0] == tok[0] and not e[2] and lo <= e[3] and e[4] <= hi)]
                hs.append((tok, q, wr, lo, hi))

    def token(q, sem, n):
        total[sem] = total.get(sem, 0) + n
        tok = (sem, total[sem])
        clock[tok] = dict(known[q])
        clock[tok][sem] = total[sem]
        return tok

    def op(q, calls, reads, writes, noself=False):
        if not isinstance(calls, list):
            calls = [calls]
        need(q, conflicts(q, reads, writes, noself))
        sem = "s" + q
        for c in calls:
            c(eng[q]).then_inc(T.sem[sem], 1)
            tok = token(q, sem, 1)
        record(tok, q, reads, writes)

    nd = [0]

    def dma(q, out, in_, reads, writes):
        need(q, conflicts(q, reads, writes, False))
        sem = "d%d" % nd[0]
        nd[0] += 1
        eng[q].dma_start(out, in_).then_inc(T.sem[sem], 16)
        record(token(q, sem, 16), q, reads, writes)

    def remote(fn, n, reads):
        need("G", conflicts("G", reads, [], False))
        fn()
        record(token("G", "ls", n), "G", reads, [])

    def arrive(sem, n, name, width):
        total[sem] = n
        clock[(sem, n)] = {sem: n}
        hist.setdefault(name, []).append(((sem, n), "R", True, 0, width))

    def finish():
        for sem, n in total.items():
            if waited.get(sem, 0) < n:
                g.wait_ge(T.sem[sem], n)

    return op, dma, remote, arrive, finish


def rank_program(g, core, T, topo):
    rank = T.rank_of(core)
    if rank is None:
        return
    n_ranks = len(T.cores)
    nxt, prv = T.cores[(rank + 1) % n_ranks], T.cores[(rank - 1) % n_ranks]
    op, dma, remote, arrive, finish = make(g, T)
    ps = [T["ps%d" % b] for b in range(8)]

    def R(name, lo=0, hi=None):
        return (name, lo, hi if hi is not None else 1 << 20)

    def ts(out, i, s1, s2, o0, o1, reads, writes):
        if s2 is None:
            op("V", lambda e: e.tensor_scalar(out, i, s1, None, o0), reads, writes)
        else:
            op("V", lambda e: e.tensor_scalar(out, i, s1, s2, o0, o1), reads, writes)

    def tt(out, a, b, o, reads, writes):
        op("V", lambda e: e.tensor_tensor(out, a, b, o), reads, writes)

    def cp(out, i, reads, writes):
        op("V", lambda e: e.tensor_copy(out, i), reads, writes)

    def act(out, i, fn, reads, writes, **kw):
        op("S", lambda e: e.activation(out, i, fn, **kw), reads, writes)

    def fill(ap, c, name):
        op("V", lambda e: e.memset(ap, c), [], [R(name)])

    def mm(specs, reads, writes):
        op("P", [lambda e, s=s: e.matmul(s[0], s[1], s[2], s[3], s[4]) for s in specs], reads, writes, noself=True)

    def group(out, pairs):
        n = len(pairs)
        return [(out, a, b, j == 0, j == n - 1) for j, (a, b) in enumerate(pairs)]

    def z(s, r):
        return T.zs[:, 144 * s + 15 - r: 144 * s + 15 - r + 128]

    def idm(s):
        return T.ids[:, 128 * s: 128 * s + 128]

    def wrapped(s, src, stop, lo=0):
        return [(z(s, r), src[:, lo + r: stop: 16]) for r in range(16)]

    dma("S", T.nxb[:], T.nx[:], [], [R("nxb")])
    dma("Y", T.xsb[:, 0:1536], T.xp[:, 0:1536], [], [R("xsb", 0, 1536)])
    dma("S", T.h0[:], T.hm[:], [], [R("h0")])
    dma("Y", T.xsb[:, 1536:3072], T.xp[:, 1536:3072], [], [R("xsb", 1536, 3072)])
    dma("S", T.kti[:], T.kt[:], [], [R("kti")])
    fill(T.tj0[:], 0.0, "tj0")
    fill(T.thi[:], 0, "thi")
    fill(T.bmr[:], 0, "bmr")

    def iota(out, pattern, base, cm, name):
        op("G", lambda e: e.iota(out, pattern, base, cm, allow_small_or_imprecise_dtypes=True), [], [R(name)])
    iota(T.pci[:], [[0, 1]], 0, 1, "pci")
    iota(T.ri[:], [[1, 192]], 0, 0, "ri")
    iota(T.ix[:], [[1, 4], [0, 48]], 0, 0, "ix")
    iota(T.idb[:], [[0, 4], [1, 48]], 0, 0, "idb")
    iota(T.im[:], [[1, 240]], 0, 0, "im")
    iota(T.kcb[:], [[0, 16], [1, 16]], 0, 0, "kcb")
    iota(T.igr[:], [[16, 8], [0, 16]], 0, 0, "igr")
    iota(T.bsi[:], [[256, 16]], 0, 0, "bsi")
    iota(T.ig64[:], [[16, 8], [0, 64]], 0, 0, "ig64")
    iota(T.ig49[:], [[16, 8], [0, 49]], 0, 0, "ig49")
    iota(T.cbw[:], [[0, 8], [1, 49]], 0, 0, "cbw")
    iota(T.pat[:], [[0, 8], [1, 64]], 0, 0, "pat")
    C = lambda j: T.cols[:, j:j + 1]
    RC = lambda j: R("cols", j, j + 1)
    CP_, CR, CG, CGZ, CRS, W0, WA, WB, WG, KD, KM, WX, TA = 0, 1, 2, 3, 4, 8, 14, 15, 16, 17, 18, 19, 24
    ts(T.ria[:], T.pci[:], 15, None, OP.bitwise_and, None, [R("pci")], [R("ria")])
    cp(C(CP_), T.pci[:], [R("pci")], [RC(CP_)])
    cp(C(CR), T.ria[:], [R("ria")], [RC(CR)])
    ts(idm(I1), T.im[:, 0:128], C(CP_), 1.0, OP.is_equal, OP.mult, [R("im"), RC(CP_)], [R("ids", 0, 128)])
    ts(C(CRS), C(CR), S16, None, OP.mult, None, [RC(CR)], [RC(CRS)])
    ts(T.j2[:, 0:192], T.ri[:], 0.0, C(CRS), OP.mult, OP.add, [R("ri"), RC(CRS)], [R("j2", 0, 192)])
    ts(T.pxd[:, 0:192], T.ix[:], S16, None, OP.mult, None, [R("ix")], [R("pxd", 0, 192)])
    ts(T.pxd[:, 192:384], T.idb[:], S16, None, OP.mult, None, [R("idb")], [R("pxd", 192, 384)])
    tjrow = []

    def to_row(q, tab, row, src, name, lo):
        key = "%sr%d" % (tab, row)
        dma(q, T[tab][row::16, :], src[:, lo:lo + 192], [R(name, lo, lo + 192), R(tab)], [R(key)])
    to_row("S", "tj0", 0, T.j2, "j2", 0)
    to_row("Y", "tj0", 1, T.pxd, "pxd", 0)
    to_row("S", "tj0", 2, T.pxd, "pxd", 192)
    ts(T.nqi[:], T.nxb[:], 1.0 / 192, -95.5 / 192, OP.mult, OP.add, [R("nxb")], [R("nqi")])
    ts(T.nx2[:, 0:192], T.nqi[:], S16, None, OP.mult, None, [R("nqi")], [R("nx2", 0, 192)])
    to_row("Y", "tj0", 3, T.nx2, "nx2", 0)
    ts(T.nt[:], T.nqi[:], -192.0, None, OP.mult, None, [R("nqi")], [R("nt")])
    tt(T.nt2[:], T.nt[:], T.nxb[:], OP.add, [R("nxb"), R("nt")], [R("nt2")])
    ts(T.nx2[:, 192:384], T.nt2[:], S16, None, OP.mult, None, [R("nt2")], [R("nx2", 192, 384)])
    to_row("Y", "tj0", 4, T.nx2, "nx2", 192)
    TJ0 = [R("tj0")] + [R("tj0r%d" % r) for r in range(5)]
    TJ1 = [R("tj1"), R("tj1r0"), R("tj1r2")]
    dma("Y", T.thi[0::16, :], T.th[:], [], [R("thi")])
    dma("Y", T.bmr[0::16, :], T.bm[:], [], [R("bmr")])
    dma("Y", T.x15[:], T.xp[15::16, :], [], [R("x15")])

    def make_hrep(h, sset, gset=(), ks=range(16)):
        for k in ks:
            o, i = T.hrep[:, k::16], T[h][:]
            if k in gset:
                op("G", lambda e: e.affine_select(o, i, [[0, 256]], OP.is_ge, 0.0, 1, 0), [R(h)], [R("hrep%d" % k)])
            elif k not in sset:
                cp(o, i, [R(h)], [R("hrep%d" % k)])
            else:
                act(o, i, FN.Copy, [R(h)], [R("hrep%d" % k)])
    HREP = [R("hrep%d" % k) for k in range(16)]
    make_hrep("h0", (0, 1, 2, 3, 5, 6, 7, 9, 10, 11, 13, 14), (4, 8, 12, 15))

    tt(C(CG), C(CP_), C(CR), OP.subtract, [RC(CP_), RC(CR)], [RC(CG)])
    ts(C(CGZ), C(CG), 15.0, None, OP.add, None, [RC(CG)], [RC(CGZ)])

    def ident(j, v):
        act(idm(j), idm(I1), FN.Copy, [R("ids", 0, 128)], [R("ids", 128 * j, 128 * j + 128)], scale=v)

    def wcol(j, terms):
        keys = []
        for n, (r, v) in enumerate(terms):
            dst = j if len(terms) == 1 else TA + n
            ts(C(dst), C(CR), float(r), v, OP.is_equal, OP.mult, [RC(CR)], [RC(dst)])
            keys.append(dst)
        if len(keys) == 3:
            tt(C(TA + 3), C(TA), C(TA + 1), OP.add, [RC(TA), RC(TA + 1)], [RC(TA + 3)])
            tt(C(j), C(TA + 3), C(TA + 2), OP.add, [RC(TA + 3), RC(TA + 2)], [RC(j)])
        elif len(keys) == 2:
            tt(C(j), C(TA), C(TA + 1), OP.add, [RC(TA), RC(TA + 1)], [RC(j)])

    def zset(s, terms):
        if terms is None:
            w, rd = 16.0, []
        else:
            if terms:
                wcol(W0 + s, terms)
            w, rd = C(W0 + s), [RC(W0 + s)]
        act(T.zs[:, 144 * s:144 * s + 144], T.zb[:], FN.Copy, [R("zb")] + rd, [R("zs", 144 * s, 144 * s + 144)], scale=w)
    ts(T.zb[:], T.im[:, 0:144], C(CGZ), None, OP.is_equal, None, [R("im"), RC(CGZ)], [R("zb")])
    Z = lambda s: R("zs", 144 * s, 144 * s + 144)
    ID = lambda s: R("ids", 128 * s, 128 * s + 128)
    zset(ZK, None)
    ts(T.bo[:], T.igr[:], C(CG), None, OP.is_equal, None, [R("igr"), RC(CG)], [R("bo")])
    ts(T.rst[:], T.kcb[:], 0.0, 1e9, OP.is_equal, OP.mult, [R("kcb")], [R("rst")])
    ts(T.r16[:], T.ria[:], 16, None, OP.mult, None, [R("ria")], [R("r16")])
    cp(C(TA + 4), T.r16[:], [R("r16")], [RC(TA + 4)])
    ts(T.bs[:], T.bsi[:], C(TA + 4), None, OP.add, None, [R("bsi"), RC(TA + 4)], [R("bs")])
    cp(T.k0[:], T.kti[:], [R("kti")], [R("k0")])
    zset(ZMA, [(3, 192 * U), (4, U)])


    def setup_count():
        wcol(WA, [(0, 4 * U), (1, U)])
        wcol(WG, [(0, 1.0)])
        wcol(WB, [(2, -U)])
        wcol(W0 + ZQ, [(0, U)])
        wcol(W0 + ZY, [(0, 192 * U), (1, 48 * U), (2, U)])
        ts(T.rha[:], T.ig64[:], C(CG), C(WA), OP.is_equal, OP.mult, [R("ig64"), RC(CG), RC(WA)], [R("rha")])
        ts(T.rhb[:], T.ig49[:], C(CG), C(WB), OP.is_equal, OP.mult, [R("ig49"), RC(CG), RC(WB)], [R("rhb")])
        act(T.cbi[:], T.cbw[:], FN.Identity, [R("cbw")], [R("cbi")], bias=-0.5)
        ts(ps[0][:, 0:392], T.ig49[:], C(CG), C(WG), OP.is_equal, OP.mult, [R("ig49"), RC(CG), RC(WG)], [R("ps0")])
        tt(T.rhg[:], T.cbi[:], ps[0][:, 0:392], OP.mult, [R("ps0"), R("cbi")], [R("rhg")])
    setup_count()

    for c in range(6):
        b = 2 + c
        sl = slice(512 * c, 512 * c + 512)
        mm(group(ps[b][:], [(idm(I1), T.xsb[:, sl]), (idm(I1), T.tj0[:, sl])]),
           [ID(I1), R("xsb", 512 * c, 512 * c + 512)] + TJ0, [R("ps%d" % b)])
        if c not in (3, 5):
            act(T.ev[:, sl], ps[b][:], FN.Copy, [R("ps%d" % b)], [R("ev", 512 * c, 512 * c + 512)])
        else:
            cp(T.ev[:, sl], ps[b][:], [R("ps%d" % b)], [R("ev", 512 * c, 512 * c + 512)])
    dma("Y", T.plw[:], T.pl[:], [R("ev")], [R("plw")])
    zset(ZQ, [])
    zset(ZY, [])

    def setup_thr():
        ts(T.bof[:], T.igr[:], C(CG), None, OP.is_equal, None, [R("igr"), RC(CG)], [R("bof")])
        cp(T.thf[:], T.thi[:], [R("thi")], [R("thf")])
        mm(group(ps[4][:, 160:162], [(T.bof[:], T.thf[:])]), [R("bof"), R("thf")], [R("ps4", 160, 162)])
        fill(T.zro[:], 0.0, "zro")
        ident(ING, -BIG)
        act(T.v15[:], T.x15[:], FN.Copy, [R("x15")], [R("v15")])
        ident(I192, 192 * U)
        ident(I1S, U)
        ident(I16, 16 * U)

    def setup_thr2():
        ts(T.thr[:, 0:1], ps[4][:, 160:161], -0.5, None, OP.add, None, [R("ps4", 160, 162)], [R("thr", 0, 1)])
        ts(T.thr[:, 2:3], ps[4][:, 160:161], -0.5, None, OP.add, None, [R("ps4", 160, 162)], [R("thr", 2, 3)])
        ts(T.thr[:, 1:2], ps[4][:, 161:162], 0.5 - BIG, None, OP.add, None, [R("ps4", 160, 162)], [R("thr", 1, 2)])

    def setup_book():
        ts(T.bqi[:], T.bmr[:], 1.0 / 192, -95.5 / 192, OP.mult, OP.add, [R("bmr")], [R("bqi")])
        ts(T.bqs[:], T.bqi[:], S16, None, OP.mult, None, [R("bqi")], [R("bqs")])
        ts(T.bt[:], T.bqi[:], -192.0, None, OP.mult, None, [R("bqi")], [R("bt")])

    def setup_book2():
        tt(T.bt2[:], T.bt[:], T.bmr[:], OP.add, [R("bt"), R("bmr")], [R("bt2")])
        ts(T.bns[:], T.bt2[:], S16, None, OP.mult, None, [R("bt2")], [R("bns")])
        mm(group(ps[4][:, 0:16], wrapped(ZY, T.bqs, 256) + wrapped(ZQ, T.bns, 256)),
           [R("bqs"), R("bns"), Z(ZQ), Z(ZY)], [R("ps4", 0, 16)])

    def setup_move():
        ts(T.pk3[:], T.pci[:], 3, None, OP.bitwise_and, None, [R("pci")], [R("pk3")])
        ts(T.pk4[:], T.pci[:], 2, None, OP.arith_shift_right, None, [R("pci")], [R("pk4")])
        cp(C(KM), T.pk3[:], [R("pk3")], [RC(KM)])
        ts(C(KD), T.pk4[:], 112.0, None, OP.add, None, [R("pk4")], [RC(KD)])
        for x in range(4):
            ts(C(WX + x), C(KM), float(x), VOID, OP.is_equal, OP.mult, [RC(KM)], [RC(WX + x)])
            ts(T.zx[:, 240 * x:240 * x + 240], T.im[:], C(KD), C(WX + x), OP.is_equal, OP.mult,
               [R("im"), RC(KD), RC(WX + x)], [R("zx")] if x == 0 else [R("zx%d" % x)])

    def setup_state():
        ts(T.j2[:, 192:384], T.ri[:], S16, None, OP.mult, None, [R("ri")], [R("j2", 192, 384)])
        tt(T.dd[:], T.nx2[:], T.j2[:], OP.subtract, [R("nx2"), R("j2")], [R("dd")])
        act(T.d2[:], T.dd[:], FN.Copy, [R("dd")], [R("d2")], scale=1.0 / VOID)

    def setup_last():
        act(T.nxu[:], T.nx2[:], FN.Copy, [R("nx2")], [R("nxu")], scale=U)
        act(T.mrow[:], T.bo[:], FN.Copy, [R("bo"), RC(W0 + ZMA)], [R("mrow")], scale=C(W0 + ZMA))

    def book():
        act(T.ry[:], T.tj0[:, 0:P].indirect(T.yl[:]), FN.Identity, TJ0 + [R("yl")], [R("ry")])

    for hop in (1, 2):
        x = len(topo.engines(prv, core))
        arrive("ah%d" % hop, x, "hl%d" % hop, 256)
        arrive("ak%d" % hop, x, "kl%d" % hop, 256)

    def send(dst, src, sem):
        rid, pid = topo.addr(nxt)[:2]
        remote(lambda: g.remote_dma(T[dst][:], T[src][:], T.sem[sem], T.sem.ls, pid, rid, topo.mask(core, nxt)),
               len(topo.engines(core, nxt)), [R(src)])

    def tj_piece(j):
        w = 24
        if t == 0:
            act(T.tj1[:, 384 * j:384 * j + 384], T.xsb[:, 384 * j:384 * j + 384], FN.Copy, [R("xsb")],
                [R("tj1", 384 * j, 384 * j + 384)], scale=0.0)
            return
        act(T.tj2[:, 16 * w * j:16 * w * (j + 1)], T.tj1[:, 0:P].indirect(T.jl[:, w * j:w * (j + 1)]), FN.Identity,
            TJ1 + [R("jl", w * j, w * (j + 1))], [R("tj2", 16 * w * j, 16 * w * (j + 1))])

    def gen(u, ba, bb):
        lo = 128 * u
        sl = slice(lo, lo + 128)
        if ba is not None:
            mm(group(ps[ba][:], [(T.rs[:, sl], T.rha[:])]), [R("rs", lo, lo + 128), R("rha")], [R("ps%d" % ba)])
        if bb is None:
            return
        mm(group(ps[bb][:, 0:392], [(T.rs[:, sl], T.rhb[:]), (T.gob[:, sl], T.rhg[:])]),
           [R("rs", lo, lo + 128), R("rhb"), R("gob", lo, lo + 128), R("rhg")], [R("ps%d" % bb)])

    def isq(u, ba):
        tt(T.oa[:, 512 * u:512 * u + 512], ps[ba][:], T.pat[:], OP.is_equal, [R("ps%d" % ba), R("pat")], [R("oa", u, u + 1)])

    def sgn(u, bb):
        act(T.sb[:, 392 * u:392 * u + 392], ps[bb][:, 0:392], FN.Sign, [R("ps%d" % bb)], [R("sb", u, u + 1)])

    def prod(u):
        mm([(ps[0][0:64, 49 * k:49 * k + 49], T.oa[:, 512 * u + 64 * k:512 * u + 64 * k + 64],
             T.sb[:, 392 * u + 49 * k:392 * u + 49 * k + 49], False, u == 5 and k == 7) for k in range(8)],
           [R("oa", u, u + 1), R("sb", u, u + 1)], [R("ps0")])

    for t in range(3):
        last = t == 2
        xt, xn = (T.ev, "ev") if t == 0 else (T.x2, "x2")
        kn = ("k0", "kl1", "kl2")[t]
        hn = ("h0", "hl1", "hl2")[t]
        if t:
            book()
        tj_piece(0), tj_piece(1)
        a0 = 0
        for c, na in enumerate((5, 4, 4, 2, 1)):
            a1 = a0 + na
            lo, hi = 256 * a0, 256 * a1
            tt(T.dw[:, lo:hi], xt[:, 0:P].indirect(T[kn][:, 16 * a0:16 * a1]), T.hrep[:, lo:hi], OP.subtract,
               [R(xn), R(kn)] + HREP, [R("dw", lo, hi)])
            act(T.ab[:, a0:a1, :], T.dw[:, lo:hi], FN.Abs, [R("dw", lo, hi)], [R("ab", a0, a1)])
            kb, klo = (0, 16 * a0) if a1 < 16 else (1, 0)
            mm(group(ps[kb][:, klo:klo + 16 * na],
                     [(idm(I1), T.kcb[:, 16 * a0:16 * a1])] + [(z(ZK, r), T.ab[:, a0:a1, 16 * r:16 * r + 16]) for r in range(16)]),
               [R("ab", a0, a1), R("kcb"), Z(ZK), ID(I1)], [R("ps%d" % kb, klo, klo + 16 * na)])
            a0 = a1
        if t == 0:
            setup_thr()
            setup_book()
        else:
            cp(T.aci[:], T.acn[:], [R("acn")], [R("aci")])
            ts(T.acj[:], T.aci[:], 31, None, OP.bitwise_and, None, [R("aci")], [R("acj")])
            tt(T.thr[:, 2:3], T.acj[:], T.thr[:, 0:1], OP.add, [R("acj"), R("thr", 0, 1)], [R("thr", 2, 3)])
        tj_piece(2), tj_piece(3)
        for kb, lo, hi in ((0, 0, 240), (1, 240, 256)):
            op("V", lambda e: e.tensor_tensor_scan(T.sc[:, lo:hi], T.rst[:, lo:hi], ps[kb][:, lo * (1 - kb):lo * (1 - kb) + hi - lo],
                                                   1e9, OP.max, OP.min), [R("rst"), R("ps%d" % kb, 0, 240)], [R("sc", lo, hi)])
        cp(T.i0[:], T.sc[:, 15::16], [R("sc")], [R("i0")])
        ts(T.i1[:], T.i0[:], 15, None, OP.bitwise_and, None, [R("i0")], [R("i1")])
        tt(T.i2[:], T.i1[:], T.bs[:], OP.add, [R("i1"), R("bs")], [R("i2")])
        cp(T.off[:], T.i2[:], [R("i2")], [R("off")])
        cp(T.w[:], T.dw[:, 0:4096].indirect(T.off[:]), [R("dw"), R("off")], [R("w")])
        zm = ZMA if t == 0 else ZMI

        def places():
            mm(group(ps[4][:, 16:64], wrapped(ZY, T.rs, 768)) + group(ps[4][:, 64:112], wrapped(ZG, T.gob, 768)),
               [R("rs"), R("gob"), Z(ZY), Z(ZG)], [R("ps4", 16, 112)])

        def pick():
            ts(T.yg[:], ps[4][:, 0:112], S16, None, OP.mult, None, [R("ps4", 0, 112)], [R("yg")])
            tt(T.ta[:], T.yg[:, 16:64], T.yg[:, 0:48], OP.subtract, [R("yg")], [R("ta")])
            tt(T.tb[:], T.ta[:], T.yg[:, 64:112], OP.mult, [R("ta"), R("yg")], [R("tb")])
            tt(T.yy1[:], T.tb[:, 0:16], T.yg[:, 0:16], OP.add, [R("tb"), R("yg")], [R("yy1")])
            tt(T.yy2[:], T.tb[:, 16:32], T.tb[:, 32:48], OP.add, [R("tb")], [R("yy2")])
            tt(T.yy3[:], T.yy1[:], T.yy2[:], OP.add, [R("yy1"), R("yy2")], [R("yy3")])
            ts(T.yl[:], T.yy3[:], U, None, OP.mult, None, [R("yy3")], [R("yl")])

        def jpart(j):
            lo = 96 * (j // 2)
            if t:
                mm(group(ps[3][:, 128 + lo + 192 * (j % 2):224 + lo + 192 * (j % 2)],
                         [(z((ZQ, ZN)[j % 2], r), T.tj2[:, 16 * lo + r:16 * lo + 1536:16]) for r in range(16)]),
                   [R("tj2", 16 * lo, 16 * lo + 1536), Z(ZQ), Z(ZN)], [R("ps3", 128, 512)])

        for s in range(3):
            c0, c1 = 256 * s, 256 * s + 256
            rsl = slice(c0, c1)
            hin = (hn, "hi0", "hi1")[s]
            hout = ("hi0", "hi1", "hs%d" % t)[s]
            act(T.a1[:], T.w[:], FN.Abs, [R("w")], [R("a1")])
            if s < 2:
                act(T.hv[:], T.w[:], FN.Identity, [R("w")], [R("hv")], bias=-0.25, scale=0.5)
            if s == 0:
                mm([(ps[0][0:64, 0:392], T.ids[:, 0:64], T.zro[:], True, False)], [ID(I1), R("zro")], [R("ps0")])
            else:
                mm([(ps[1][:, 0:256], idm(ING), T.gob[:, c0 - 256:c0], True, False)], [R("gob", c0 - 256, c0), ID(ING)], [R("ps1")])
            if t or s == 0:
                ts(ps[6][:, 0:256], T.w[:], MAGIC, MAGIC, OP.add, OP.subtract, [R("w")], [R("ps6", 0, 256)])
                tt(T.rs[:, rsl], T.w[:], ps[6][:, 0:256], OP.subtract, [R("w"), R("ps6", 0, 256)], [R("rs", c0, c1)])
            mm([(ps[1][:, 0:256], T.bo[:], T.a1[:], s == 0, True)], [R("a1"), R("bo")], [R("ps1")])
            if s < 2:
                mm(group(ps[4][:, 192:208], wrapped(zm, T.rs, c1, c0)), [R("rs", c0, c1), Z(zm)], [R("ps4", 192, 208)])
                if t and s == 0:
                    mm(group(ps[4][:, 128:144], wrapped(ZMI, T.ry, 256)), [R("ry"), Z(ZMI)], [R("ps4", 128, 144)])
                    jpart(0)
            else:
                ts(T.qb[:], T.w[:], 0.5, -0.25, OP.mult, OP.add, [R("w")], [R("qb")])
            if t == 0 and s == 0:
                setup_thr2()
            qq, qn = (T.hv, "hv") if s < 2 else (T.qb, "qb")
            if s:
                isq(2 * s - 2, 5)
                sgn(2 * s - 2, 7)
            if t == 0 and s == 2:
                setup_last()
            tj_piece(4 + s)
            if s == 2:
                tj_piece(7)
            th = T.thr[:, 2:3] if s == 0 else T.thr[:, 1:2]
            ts(ps[2][:, 0:256], ps[1][:, 0:256], th, None, OP.is_le, None, [R("ps1"), R("thr", 1, 3)], [R("ps2", 0, 256)])
            tt(ps[2][:, 256:512], qq[:], ps[2][:, 0:256], OP.mult, [R(qn), R("ps2", 0, 256)], [R("ps2", 256, 512)])
            tt(T[hout][:], T[hin][:], ps[2][:, 256:512], OP.add, [R(hin), R("ps2", 256, 512)], [R(hout)])
            if s < 2:
                cp(T.ml[:], ps[4][:, 192:208], [R("ps4", 192, 208)], [R("ml")])
            if s == 0:
                act(T.gob[:, rsl], ps[2][:, 0:256], FN.Copy, [R("ps2", 0, 256)], [R("gob", c0, c1), R("acn")], accum_out=T.acn[:])
            else:
                act(T.gob[:, rsl], ps[2][:, 0:256], FN.Copy, [R("ps2", 0, 256)], [R("gob", c0, c1)])
            if t == 0 and s < 2:
                act(T.rs[:, c1:c1 + 256], T.tj0[:, 0:P].indirect(T.ml[:]), FN.Identity, TJ0 + [R("ml")], [R("rs", c1, c1 + 256)])
            if s < 2:
                tt(T.w[:], xt[:, 0:P].indirect(T.ml[:]), T[hout][:], OP.subtract, [R(xn), R("ml"), R(hout)], [R("w")])
            if s == 1:
                jpart(1)
            if s:
                gen(2 * s - 1, 5, 7)
                if s == 2:
                    gen(5, 6, None)
                    jpart(2)
                prod(2 * s - 2)
                isq(2 * s - 1, 5)
                sgn(2 * s - 1, 7)
            gen(2 * s, 5, 7)
            if t and s == 1:
                cp(T.bl[:], ps[4][:, 128:144], [R("ps4", 128, 144)], [R("bl")])
            if s:
                prod(2 * s - 1)
        gen(5, None, 1)
        if not last:
            send("hl%d" % (t + 1), "hs%d" % t, "ah%d" % (t + 1))
        else:
            dma("Y", T.yh[:], T.hs2[:], [R("hs2")], [R("yh")])
        isq(5, 6)
        isq(4, 5)
        sgn(4, 7)
        prod(4)
        sgn(5, 1)
        prod(5)
        jpart(3)
        if t == 0:
            setup_book2()
            setup_move()
        act(T.sgc[0:64, 0:392], ps[0][0:64, 0:392], FN.Copy, [R("ps0")], [R("sgc")])
        tt(T.flg[0:64, 0:391], ps[0][0:64, 1:392], T.sgc[0:64, 0:391], OP.is_gt, [R("ps0"), R("sgc")], [R("flg")])
        for x in range(4):
            mm(group(ps[5][:, 48 * x:48 * x + 48], [(T.zx[0:64, 240 * x + 112 - 16 * k:240 * x + 240 - 16 * k],
                                                     T.flg[0:64, 49 * k:49 * k + 48]) for k in range(8)]),
               [R("flg"), R("zx")] + [R("zx%d" % i) for i in (1, 2, 3)], [R("ps5", 48 * x, 48 * x + 48)])
        if t:
            tt(T.dd[:], T.nxu[:], ps[3][:, 128:512], OP.subtract, [R("nxu"), R("ps3", 128, 512)], [R("dd")])
            act(T.d2[:], T.dd[:], FN.Copy, [R("dd")], [R("d2")], scale=S16 / VOID)
            act(T.j2[:], ps[3][:, 128:512], FN.Copy, [R("ps3", 128, 512)], [R("j2")], scale=S16)
            act(T.rb[:], T.tj2[:, 0:P].indirect(T.bl[:]), FN.Identity, [R("tj2"), R("bl")], [R("rb")])

        else:
            setup_state()
        places()
        if not last:
            tt(T.v15[:], T.v15[:], ps[5][:, 0:192], OP.add, [R("v15"), R("ps5")], [R("v15")])
            dma("Y", T.ev[15::16, :], T.v15[:], [R("v15")], [R("ev")])
        tt(ps[2][:, 0:192], T.d2[:, 0:192], ps[5][:, 0:192], OP.mult, [R("d2"), R("ps5")], [R("ps2", 0, 192)])
        tt(ps[2][:, 192:384], T.d2[:, 192:384], ps[5][:, 0:192], OP.mult, [R("d2"), R("ps5")], [R("ps2", 192, 384)])
        tt(T.j2n[:], T.j2[:], ps[2][:, 0:384], OP.add, [R("j2"), R("ps2", 0, 384)], [R("j2n")])
        to_row("Y", "tj1", 0, T.j2n, "j2n", 0)
        to_row("Y", "tj1", 2, T.j2n, "j2n", 192)
        mm(group(ps[3][:, 128:320], [(idm(I192), T.j2n[:, 0:192]), (idm(I1S), T.j2n[:, 192:384])])
           + group(ps[3][:, 320:512], [(idm(I1S), T.j2n[:, 0:192]), (idm(I16), T.j2n[:, 192:384])]),
           [R("j2n"), ID(I192), ID(I1S), ID(I16)], [R("ps3", 128, 512)])
        if t:
            mm(group(ps[4][:, 0:16], wrapped(ZY, T.rb, 256)), [R("rb"), Z(ZY)], [R("ps4", 0, 16)])
        if t == 0:
            wcol(W0 + ZMI, [(3, U), (4, 16 * U)])
            wcol(W0 + ZN, [(2, U)])
        cp(T.jl[:], ps[3][:, 128:512], [R("ps3", 128, 512)], [R("jl")])
        pick()
        if not last:
            make_hrep("hl%d" % (t + 1), (2, 4, 7, 10, 12, 14), (0, 3, 6, 9, 13), (0, 2, 3, 4, 6, 7, 9, 10, 12, 13, 14))
            if t == 0:
                zset(ZMI, [])
                zset(ZN, [])
            ts(T.g16[:], T.plw[:, 0:P].indirect(T.yl[:]), 16.0, None, OP.mult, None, [R("plw"), R("yl")], [R("g16")])
            ts(T.kq[:], T.g16[:], 1.0 / 3072, -1528.0 / 3072, OP.mult, OP.add, [R("g16")], [R("kq")])
            ts(ps[6][:, 0:256], T.kq[:], -3071.0, None, OP.mult, None, [R("kq")], [R("ps6", 0, 256)])
            tt(T.kk[:], T.g16[:], ps[6][:, 0:256], OP.add, [R("g16"), R("ps6", 0, 256)], [R("kk")])
            cp(T["ks%d" % t][:], T.kk[:], [R("kk")], [R("ks%d" % t)])
            send("kl%d" % (t + 1), "ks%d" % t, "ak%d" % (t + 1))
            make_hrep("hl%d" % (t + 1), (), (1, 5, 8, 11, 15), (1, 5, 8, 11, 15))

            def through(src, sn, dst, dn, lo, nv):
                op("V", lambda e: e.tensor_copy(dst[:, 0:16 * nv], src[:, 0:P].indirect(T.jl[:, lo:lo + nv])),
                   [R(sn), R("jl", lo, lo + nv)], [R(dn, 0, 16 * nv)])
                act(dst[:, 16 * nv:3072], src[:, 0:P].indirect(T.jl[:, lo + nv:lo + 192]), FN.Identity,
                    [R(sn), R("jl", lo + nv, lo + 192)], [R(dn, 16 * nv, 3072)])
            through(T.ev, "ev", T.x1, "x1", 0, 60)
            through(T.x1, "x1", T.x2, "x2", 192, 96)

        else:
            for lo in (0, 48):
                b = lo + 96
                cp(T.tj2[:, 16 * lo:16 * lo + 768], T.tj1[:, 0:P].indirect(T.jl[:, lo:lo + 48]),
                   TJ1 + [R("jl", lo, lo + 48)], [R("tj2", 16 * lo, 16 * lo + 768)])
                act(T.tj2[:, 16 * b:16 * b + 768], T.tj1[:, 0:P].indirect(T.jl[:, b:b + 48]), FN.Identity,
                    TJ1 + [R("jl", b, b + 48)], [R("tj2", 16 * b, 16 * b + 768)])
                for c in (lo, b):
                    mm(group(ps[7][:, c:c + 48], [(z(ZY, r), T.tj2[:, 16 * c + r:16 * c + 768:16]) for r in range(16)]),
                       [R("tj2", 16 * c, 16 * c + 768), Z(ZY)], [R("ps7", c, c + 48)])
            cp(T.yjs[:], ps[7][:, 0:192], [R("ps7")], [R("yjs")])
            dma("Y", T.yj[:], T.yjs[:], [R("yjs")], [R("yj")])
            book()
            mm(group(ps[1][:, 0:256], [(T.mrow[:], T.ry[:])]), [R("mrow"), R("ry")], [R("ps1")])
            act(T.ybs[:], ps[1][:, 0:256], FN.Copy, [R("ps1")], [R("ybs")])
            dma("S", T.yb[:], T.ybs[0::16, :], [R("ybs")], [R("yb")])
    finish()
